import numpy as np
import ml_dtypes


def mxq(x, axis, fmt="e4m3"):
    dtype, down = {"e4m3": (ml_dtypes.float8_e4m3fn, 7), "e5m2": (ml_dtypes.float8_e5m2, 14)}[fmt]
    v = np.moveaxis(np.asarray(x, np.float32).astype(ml_dtypes.bfloat16).astype(np.float64), axis, -1)
    blocks = v.reshape(v.shape[:-1] + (-1, 32))
    amax = np.abs(blocks).max(-1, keepdims=True)
    byte = np.maximum(np.where(amax > 0, np.frexp(amax)[1] - 1 + 127, 0) - down, 1)
    scale = np.exp2(byte - 127.0)
    codes = (blocks / scale).astype(np.float32).astype(dtype).astype(np.float64)
    return np.moveaxis((codes * scale).reshape(v.shape), -1, axis)


WIDE = False


def mx_kscale(k):
    if not WIDE:
        return np.ones(k)
    levels = np.array([24, -24, 12, -12, 0])
    if k % 512:
        return np.exp2(np.random.permutation(np.resize(levels, k // 32))).repeat(32)
    a = np.empty((k // 512, 16))
    for p in range(k // 512):
        a[p, :8] = np.random.permutation(np.resize(levels, 8))
        for g in range(8):
            far = levels[np.abs(levels - a[p, g]) >= 10]
            a[p, g + 8] = far[np.random.randint(len(far))]
    return np.exp2(a.ravel()).repeat(32)


def f64(x):
    return np.asarray(x).astype(np.float64)


def striped(idx):
    return np.tile(idx.reshape(-1, 16).T, (8, 1)).astype(np.uint16)


def unstriped(offs):
    return offs[:16].T.reshape(-1).astype(np.int64)


E2M1 = np.array([0.0, 0.5, 1.0, 1.5, 2.0, 3.0, 4.0, 6.0, -0.0, -0.5, -1.0, -1.5, -2.0, -3.0, -4.0, -6.0])


def pack_weight(w, fmt):
    k, n = w.shape
    w = f64(np.asarray(w, np.float32).astype(ml_dtypes.bfloat16)).reshape(k // 32, 32, n)
    amax = np.abs(w).max(1)
    if fmt == "e4m3":
        byte = np.frexp(amax)[1] - 1 + 127 - 7
    else:
        mant, ex = np.frexp(amax / 6.0)
        byte = np.where(mant > 0.5, ex, ex - 1) + 127
    byte = np.clip(np.where(amax > 0, byte, 1), 1, 254)
    scaled = (w * np.exp2(127.0 - byte)[:, None, :]).reshape(k, n).astype(np.float32)
    by_word = np.ascontiguousarray(scaled.reshape(k // 512, 128, 4, n).transpose(0, 1, 3, 2))
    if fmt == "e4m3":
        words = by_word.astype(ml_dtypes.float8_e4m3fn).view(np.uint8)
    else:
        c = by_word.astype(ml_dtypes.float4_e2m1fn).view(np.uint8) & 0xF
        words = (c[..., 0::2] | (c[..., 1::2] << 4)).reshape(k // 512, 128, 2 * n)
    return np.ascontiguousarray(words), np.ascontiguousarray(byte.astype(np.uint8).reshape(k // 512, 16, n))


def unpack_weight(words, scales, fmt):
    g, _, n = scales.shape
    words = np.ascontiguousarray(words).reshape(g, 128, n, -1)
    if fmt == "e4m3":
        vals = words.view(ml_dtypes.float8_e4m3fn).astype(np.float64)
    else:
        nib = np.empty((g, 128, n, 4), np.uint8)
        nib[..., 0::2] = words & 0xF
        nib[..., 1::2] = words >> 4
        vals = E2M1[nib]
    vals = vals * np.repeat(np.exp2(scales.astype(np.float64) - 127.0), 8, axis=1)[..., None]
    return vals.transpose(0, 1, 3, 2).reshape(g * 512, n)


def pack_table4(v):
    words, scales = pack_weight(v, "e2m1")
    g, t = words.shape[0] // 2, v.shape[1]
    return np.ascontiguousarray(words.reshape(g, 2, 128, t, 2).transpose(0, 2, 3, 1, 4).reshape(g, 128, t, 4)), scales


def unpack_table4(words, scales):
    g, _, t, _ = words.shape
    return unpack_weight(words.reshape(g, 128, t, 2, 2).transpose(0, 3, 1, 2, 4).reshape(2 * g, 128, 2 * t), scales, "e2m1")


def sigm(f):
    return 1.0 / (1.0 + np.exp(-np.maximum(f, -700.0)))


K, L, R, N, T, J = 512, 1024, 512, 256, 2048, 1024


def setup_inputs():
    n = np.random.standard_normal
    s = mx_kscale(K)[:, None]
    s2 = mx_kscale(L)[:, None]
    u = mx_kscale(R)[:, None]
    p_tab = pack_weight(n((K, T)) * s, "e4m3")
    p_tab2 = pack_table4(n((L, T)) * s2)
    p_wer = pack_weight(n((K, R)) / np.sqrt(K) / s * u.T, "e4m3")
    p_wei = pack_weight(n((K, R)) / np.sqrt(K) / s * u.T, "e4m3")
    p_nr = pack_weight(n((R, N)) / np.sqrt(R) / u, "e2m1")
    p_ni = pack_weight(n((R, N)) / np.sqrt(R) / u, "e2m1")
    return {
        "tab_words": p_tab[0],
        "tab_scales": p_tab[1],
        "tab2_words": p_tab2[0],
        "tab2_scales": p_tab2[1],
        "wer_words": p_wer[0],
        "wer_scales": p_wer[1],
        "wei_words": p_wei[0],
        "wei_scales": p_wei[1],
        "wrr": (n((L, R)) / np.sqrt(L) / s2).astype(np.float32),
        "wri": (n((L, R)) / np.sqrt(L) / s2).astype(np.float32),
        "nr_words": p_nr[0],
        "nr_scales": p_nr[1],
        "ni_words": p_ni[0],
        "ni_scales": p_ni[1],
        "offs": striped(np.random.permutation(T)[:J]),
        "offs2": striped(np.random.permutation(T)[:J]),
    }


def reference(tab_words, tab_scales, tab2_words, tab2_scales, wer_words, wer_scales, wei_words, wei_scales, wrr, wri, nr_words, nr_scales, ni_words, ni_scales, offs, offs2):
    idx = unstriped(offs)
    idx2 = unstriped(offs2)
    tab_ = unpack_weight(tab_words, tab_scales, "e4m3")[:, idx]
    tab2_ = unpack_table4(tab2_words, tab2_scales)[:, idx2]
    wer_ = unpack_weight(wer_words, wer_scales, "e4m3")
    aer = wer_.T @ tab_
    wei_ = unpack_weight(wei_words, wei_scales, "e4m3")
    aei = wei_.T @ tab_
    wrr_ = mxq(f64(wrr), 0, "e4m3")
    arr = wrr_.T @ tab2_
    wri_ = mxq(f64(wri), 0, "e4m3")
    ari = wri_.T @ tab2_
    hr = aer * arr - aei * ari
    hi = aer * ari + aei * arr
    hr_ = mxq(hr, 0, "e4m3")
    hi_ = mxq(hi, 0, "e4m3")
    nr_ = unpack_weight(nr_words, nr_scales, "e2m1")
    ni_ = unpack_weight(ni_words, ni_scales, "e2m1")
    y = nr_.T @ hr_ + ni_.T @ hi_
    return sigm(y)

@@ -1,0 +1,241 @@
+from contextlib import ExitStack
+
+import concourse.mybir as mybir
+
+K, L, R, N, T, J = 512, 1024, 512, 256, 2048, 1024
+FLOPS = 2 * J * (2 * K * R + 2 * L * R + 2 * R * N)
+
+F32 = mybir.dt.float32
+BF16 = mybir.dt.bfloat16
+I32 = mybir.dt.int32
+U32 = mybir.dt.uint32
+U16 = mybir.dt.uint16
+U8 = mybir.dt.uint8
+FP8X4 = mybir.dt.float8_e4m3fn_x4
+FP4X4 = mybir.dt.float4_e2m1fn_x4
+MULT = mybir.AluOpType.mult
+ADD = mybir.AluOpType.add
+SUB = mybir.AluOpType.subtract
+SIGMOID = mybir.ActivationFunctionType.Sigmoid
+
+P = 128
+CH = 128
+NCH = J // CH
+HALF = J // 2
+LAG = 1
+VECTOR_ADD_CHUNKS = 1
+
+
+def tile_list_ckg_sig_kernel(
+    tc, tab_words, tab_scales, tab2_words, tab2_scales, wer_words, wer_scales, wei_words, wei_scales,
+    wrr, wri, nr_words, nr_scales, ni_words, ni_scales, offs, offs2, out,
+):
+    nc = tc.nc
+    with ExitStack() as ctx:
+        keep = ctx.enter_context(tc.tile_pool(name="keep", bufs=1))
+        ring = ctx.enter_context(tc.tile_pool(name="ring", bufs=3))
+        psum = ctx.enter_context(tc.psum_pool(name="psum", bufs=2))
+
+        def kept(shape, dtype, name):
+            return keep.tile(shape, dtype, name=name, align_bytes=64)
+
+        list1 = keep.tile([P, J // 16], U16, name="list1")
+        list2 = keep.tile([P, J // 16], U16, name="list2")
+        tab_w = kept([P, T], U32, "tab_w")
+        tab_s = kept([P, T], U8, "tab_s")
+        tab2_w = kept([P, T], U32, "tab2_w")
+        tab2_s = kept([P, T], U8, "tab2_s")
+        we_w = kept([P, 2, R], I32, "we_w")
+        we_s = kept([P, R], U8, "we_s")
+        n_w = kept([P, 2, 2 * N], U8, "n_w")
+        n_s = kept([P, 2, N], U8, "n_s")
+        raw = [kept([P, 4, R], F32, f"raw{i}") for i in range(4)]
+        v2_s1 = kept([P, J], U8, "v2_s1")
+
+        nc.vector.memset(tab_s[:].bitcast(I32), 0)
+        nc.vector.memset(tab2_s[:].bitcast(I32), 0)
+        nc.vector.memset(we_s[:].bitcast(I32), 0)
+        nc.gpsimd.memset(n_s[:].rearrange("p a n -> p (a n)").bitcast(I32), 0)
+        nc.gpsimd.memset(v2_s1[:].bitcast(I32), 0)
+
+        def load_words(dst, words):
+            nc.sync.dma_start(out=dst, in_=words[0].rearrange("p c i -> p (c i)").bitcast(I32))
+
+        def load_weight(i):
+            w = (wrr, wri)[i // 2]
+            a = i % 2
+            nc.sync.dma_start(out=raw[i][:], in_=w[512 * a : 512 * (a + 1), :].rearrange("(p j) c -> p j c", j=4))
+
+        def load_rows(dst, first, count, rows):
+            nc.sync.dma_start(out=dst[first : first + count, :].bitcast(I32), in_=rows.bitcast(I32))
+
+        nc.sync.dma_start(list1[:], offs)
+        nc.sync.dma_start(list2[:], offs2)
+        load_weight(0)
+        for q in range(4):
+            load_rows(tab_s, 32 * q, 4, tab_scales[0, 4 * q : 4 * q + 4, :])
+        load_weight(1)
+        for q in range(4):
+            load_rows(tab2_s, 32 * q, 8, tab2_scales[:, 4 * q : 4 * q + 4, :])
+        load_weight(2)
+        for q in range(4):
+            load_rows(we_s, 32 * q, 4, wer_scales[0, 4 * q : 4 * q + 4, :])
+        load_words(we_w[:, 0, :], wer_words)
+        load_words(we_w[:, 1, :], wei_words)
+        for q in range(4):
+            load_rows(we_s, 32 * q + 4, 4, wei_scales[0, 4 * q : 4 * q + 4, :])
+        load_words(tab_w[:].bitcast(I32), tab_words)
+        load_words(tab2_w[:].bitcast(I32), tab2_words)
+        load_weight(3)
+        for e, (words, scales) in enumerate(((nr_words, nr_scales), (ni_words, ni_scales))):
+            nc.sync.dma_start(out=n_w[:, e, :].bitcast(I32), in_=words[0].bitcast(I32))
+            for q in range(4):
+                nc.gpsimd.dma_start(out=n_s[32 * q : 32 * q + 4, e, :].bitcast(I32), in_=scales[0, 4 * q : 4 * q + 4, :].bitcast(I32))
+
+        v_s = kept([P, J], U8, "v_s")
+        v_w = [kept([P, HALF], U32, f"v_w{h}") for h in range(2)]
+        v2_s0 = kept([P, J], U8, "v2_s0")
+        v2_both = [kept([P, HALF], U32, f"v2_both{h}") for h in range(2)]
+        v2_w = [kept([P, 2, HALF], U16, f"v2_w{h}") for h in range(2)]
+        we_wp = kept([P, 2, 4, P], I32, "we_wp")
+        we_sp = kept([P, 4, P], U8, "we_sp")
+        hc = HALF // 16
+
+        grouped = [kept([P, 4, P, 4], BF16, f"grouped{i}") for i in range(4)]
+        wr_w = [kept([P, 4, P], U32, f"wr_w{i}") for i in range(4)]
+        wr_s = [kept([P, 4, P], U8, f"wr_s{i}") for i in range(4)]
+
+        def cast(i, t0, t1, on_vector):
+            dst = grouped[i][:, t0:t1, :, :].rearrange("p t m j -> p m t j")
+            src = raw[i][:].rearrange("p j (m t) -> p m t j", t=4)[:, :, t0:t1, :]
+            if on_vector:
+                nc.vector.tensor_copy(out=dst, in_=src)
+            else:
+                nc.scalar.copy(out=dst, in_=src)
+
+        def quantize_weight(i, t0, t1):
+            nc.vector.quantize_mx(
+                out=wr_w[i][:, t0:t1, :].rearrange("p t m -> p (t m)").bitcast(FP8X4),
+                scales=wr_s[i][:, t0:t1, :].rearrange("p t m -> p (t m)"),
+                in_=grouped[i][:, t0:t1, :, :].rearrange("p t m j -> p (t m j)"),
+            )
+
+        def gather_table2(h):
+            nc.vector.tensor_copy(v2_both[h][:], tab2_w[:].indirect(list2[:, h * hc : (h + 1) * hc]))
+            nc.vector.tensor_copy(out=v2_w[h][:], in_=v2_both[h][:].bitcast(U16).rearrange("p (j d) -> p d j", d=2))
+
+        ae = {}
+
+        def entity(c):
+            h, c0 = divmod(c * CH, HALF)
+            ae[c] = ring.tile([P, 2, CH, 4], F32, name="ae", bufs=2)
+            for e in range(2):
+                bank = psum.tile([P, 4, CH], F32, name="ae_bank")
+                for t in range(4):
+                    nc.tensor.matmul_mx(
+                        out=bank[:, t, :],
+                        lhsT=we_wp[:, e, t, :].bitcast(FP8X4),
+                        lhsT_scale=we_sp[4 * e :, t, :],
+                        rhs=v_w[h][:, c0 : c0 + CH].bitcast(FP8X4),
+                        rhs_scale=v_s[:, c * CH : (c + 1) * CH],
+                        start=True,
+                        stop=True,
+                    )
+                nc.scalar.copy(out=ae[c][:, e, :, :], in_=bank[:].rearrange("p t j -> p j t"))
+
+        def products(c, e):
+            h, c0 = divmod(c * CH, HALF)
+            bank = psum.tile([P, 4, CH], F32, name=f"ar_bank{e}")
+            for t in range(4):
+                for a in range(2):
+                    nc.tensor.matmul_mx(
+                        out=bank[:, t, :],
+                        lhsT=wr_w[2 * e + a][:, t, :].bitcast(FP8X4),
+                        lhsT_scale=wr_s[2 * e + a][:, t, :],
+                        rhs=v2_w[h][:, a, c0 : c0 + CH].bitcast(FP4X4),
+                        rhs_scale=(v2_s0, v2_s1)[a][:, c * CH : (c + 1) * CH],
+                        start=(a == 0),
+                        stop=(a == 1),
+                    )
+            prod = ring.tile([P, 2, CH, 4], F32, name=f"prod{e}")
+            nc.vector.tensor_tensor(
+                out=prod[:],
+                in0=bank[:].rearrange("p t j -> p j t").unsqueeze(1).to_broadcast([P, 2, CH, 4]),
+                in1=ae[c][:],
+                op=MULT,
+            )
+            return prod
+
+        def combine(c, pr, pi):
+            eng = nc.vector if c >= NCH - VECTOR_ADD_CHUNKS else nc.gpsimd
+            hb = ring.tile([P, 2, CH, 4], BF16, name="hb", align_bytes=64)
+            eng.tensor_tensor(out=hb[:, 0], in0=pr[:, 0], in1=pi[:, 1], op=SUB)
+            eng.tensor_tensor(out=hb[:, 1], in0=pr[:, 1], in1=pi[:, 0], op=ADD)
+            return hb
+
+        out_v = out.rearrange("(g p) j -> p g j", p=P)
+
+        def score(c, hb):
+            h_w = ring.tile([P, 2, CH], U32, name="h_w", align_bytes=64)
+            h_s = ring.tile([P, 2, CH], U8, name="h_s", align_bytes=64)
+            nc.vector.quantize_mx(
+                out=h_w[:].rearrange("p e j -> p (e j)").bitcast(FP8X4),
+                scales=h_s[:].rearrange("p e j -> p (e j)"),
+                in_=hb[:].rearrange("p e j t -> p (e j t)"),
+            )
+            bank = psum.tile([P, 2, CH], F32, name="y_bank")
+            for g in range(2):
+                for e in range(2):
+                    nc.tensor.matmul_mx(
+                        out=bank[:, g, :],
+                        lhsT=n_w[:, e, 2 * P * g : 2 * P * (g + 1)].bitcast(FP4X4),
+                        lhsT_scale=n_s[:, e, P * g : P * (g + 1)],
+                        rhs=h_w[:, e, :].bitcast(FP8X4),
+                        rhs_scale=h_s[:, e, :],
+                        start=(e == 0),
+                        stop=(e == 1),
+                    )
+            res = ring.tile([P, 2, CH], F32, name="res")
+            nc.scalar.activation(out=res[:], in_=bank[:], func=SIGMOID)
+            nc.sync.dma_start(out=out_v[:, :, c * CH : (c + 1) * CH], in_=res[:])
+
+        def gather_table1(h):
+            nc.vector.tensor_copy(v_w[h][:], tab_w[:].indirect(list1[:, h * hc : (h + 1) * hc]))
+
+        nc.vector.tensor_copy(v_s[:], tab_s[:].indirect(list1[:]))
+        nc.vector.tensor_copy(v2_s0[:], tab2_s[:].indirect(list2[:]))
+        nc.gpsimd.dma_start(out=v2_s1[0:100, :].bitcast(I32), in_=v2_s0[4:104, :].bitcast(I32))
+        cast(0, 0, 4, False)
+        cast(1, 0, 4, False)
+        cast(2, 0, 4, False)
+        quantize_weight(0, 0, 4)
+        quantize_weight(1, 0, 4)
+        nc.vector.tensor_copy(out=we_sp[:], in_=we_s[:].rearrange("p (m t) -> p t m", t=4))
+        nc.vector.tensor_copy(
+            out=we_wp[:].rearrange("p e t m -> p e m t"), in_=we_w[:].rearrange("p e (m t) -> p e m t", t=4)
+        )
+        gather_table1(0)
+        entity(0)
+        entity(1)
+        gather_table1(1)
+        gather_table2(0)
+        quantize_weight(2, 0, 4)
+        cast(3, 0, 2, False)
+        cast(3, 2, 4, False)
+        early = [products(0, 0)]
+        quantize_weight(3, 0, 2)
+        quantize_weight(3, 2, 4)
+        early.append(products(1, 0))
+        gather_table2(1)
+
+        pending = []
+        for c in range(NCH):
+            pr = early[c] if c < len(early) else products(c, 0)
+            pi = products(c, 1)
+            if c + 2 < NCH:
+                entity(c + 2)
+            pending.append((c, combine(c, pr, pi)))
+            if len(pending) > LAG:
+                score(*pending.pop(0))
+        for item in pending:
+            score(*item)

@@ -22,7 +22,7 @@ P = 128
 CH = 128
 NCH = J // CH
 HALF = J // 2
-LAG = 1
+LAG = 2
 VECTOR_ADD_CHUNKS = 1
 
 
@@ -46,17 +46,12 @@ def tile_list_ckg_sig_kernel(
         tab2_w = kept([P, T], U32, "tab2_w")
         tab2_s = kept([P, T], U8, "tab2_s")
         we_w = kept([P, 2, R], I32, "we_w")
-        we_s = kept([P, R], U8, "we_s")
-        n_w = kept([P, 2, 2 * N], U8, "n_w")
-        n_s = kept([P, 2, N], U8, "n_s")
-        raw = [kept([P, 4, R], F32, f"raw{i}") for i in range(4)]
-        v2_s1 = kept([P, J], U8, "v2_s1")
+        we_s = keep.tile([P, R], U8, name="we_s", tag="we_s", align_bytes=64)
+        raw = [keep.tile([P, 4, R], F32, name=f"raw{i}", tag=f"raw{i}", align_bytes=64) for i in range(4)]
 
         nc.vector.memset(tab_s[:].bitcast(I32), 0)
         nc.vector.memset(tab2_s[:].bitcast(I32), 0)
         nc.vector.memset(we_s[:].bitcast(I32), 0)
-        nc.gpsimd.memset(n_s[:].rearrange("p a n -> p (a n)").bitcast(I32), 0)
-        nc.gpsimd.memset(v2_s1[:].bitcast(I32), 0)
 
         def load_words(dst, words):
             nc.sync.dma_start(out=dst, in_=words[0].rearrange("p c i -> p (c i)").bitcast(I32))
@@ -77,26 +72,22 @@ def tile_list_ckg_sig_kernel(
         load_weight(1)
         for q in range(4):
             load_rows(tab2_s, 32 * q, 8, tab2_scales[:, 4 * q : 4 * q + 4, :])
-        load_weight(2)
+        load_words(tab_w[:].bitcast(I32), tab_words)
         for q in range(4):
             load_rows(we_s, 32 * q, 4, wer_scales[0, 4 * q : 4 * q + 4, :])
         load_words(we_w[:, 0, :], wer_words)
         load_words(we_w[:, 1, :], wei_words)
+        load_weight(2)
         for q in range(4):
             load_rows(we_s, 32 * q + 4, 4, wei_scales[0, 4 * q : 4 * q + 4, :])
-        load_words(tab_w[:].bitcast(I32), tab_words)
         load_words(tab2_w[:].bitcast(I32), tab2_words)
         load_weight(3)
-        for e, (words, scales) in enumerate(((nr_words, nr_scales), (ni_words, ni_scales))):
-            nc.sync.dma_start(out=n_w[:, e, :].bitcast(I32), in_=words[0].bitcast(I32))
-            for q in range(4):
-                nc.gpsimd.dma_start(out=n_s[32 * q : 32 * q + 4, e, :].bitcast(I32), in_=scales[0, 4 * q : 4 * q + 4, :].bitcast(I32))
 
         v_s = kept([P, J], U8, "v_s")
-        v_w = [kept([P, HALF], U32, f"v_w{h}") for h in range(2)]
+        v_w = {}
         v2_s0 = kept([P, J], U8, "v2_s0")
-        v2_both = [kept([P, HALF], U32, f"v2_both{h}") for h in range(2)]
-        v2_w = [kept([P, 2, HALF], U16, f"v2_w{h}") for h in range(2)]
+        v2_both = {}
+        v2_w = {}
         we_wp = kept([P, 2, 4, P], I32, "we_wp")
         we_sp = kept([P, 4, P], U8, "we_sp")
         hc = HALF // 16
@@ -121,6 +112,8 @@ def tile_list_ckg_sig_kernel(
             )
 
         def gather_table2(h):
+            v2_both[h] = keep.tile([P, HALF], U32, name="v2_both", tag="we_s", align_bytes=64)
+            v2_w[h] = ring.tile([P, 2, HALF], U16, name="v2_w", bufs=2, align_bytes=64)
             nc.vector.tensor_copy(v2_both[h][:], tab2_w[:].indirect(list2[:, h * hc : (h + 1) * hc]))
             nc.vector.tensor_copy(out=v2_w[h][:], in_=v2_both[h][:].bitcast(U16).rearrange("p (j d) -> p d j", d=2))
 
@@ -200,38 +193,49 @@ def tile_list_ckg_sig_kernel(
             nc.sync.dma_start(out=out_v[:, :, c * CH : (c + 1) * CH], in_=res[:])
 
         def gather_table1(h):
+            v_w[h] = ring.tile([P, HALF], U32, name="v_w", bufs=2, align_bytes=64)
             nc.vector.tensor_copy(v_w[h][:], tab_w[:].indirect(list1[:, h * hc : (h + 1) * hc]))
 
         nc.vector.tensor_copy(v_s[:], tab_s[:].indirect(list1[:]))
         nc.vector.tensor_copy(v2_s0[:], tab2_s[:].indirect(list2[:]))
-        nc.gpsimd.dma_start(out=v2_s1[0:100, :].bitcast(I32), in_=v2_s0[4:104, :].bitcast(I32))
         cast(0, 0, 4, False)
         cast(1, 0, 4, False)
-        cast(2, 0, 4, False)
+        v2_s1 = keep.tile([P, J], U8, name="v2_s1", tag="raw1", align_bytes=64)
+        nc.gpsimd.memset(v2_s1[96:128, :].bitcast(I32), 0)
+        nc.sync.dma_start(out=v2_s1[0:100, :].bitcast(I32), in_=v2_s0[4:104, :].bitcast(I32))
         quantize_weight(0, 0, 4)
+        gather_table1(0)
+        nc.vector.tensor_copy(
+            out=we_wp[:].rearrange("p e t (g i) -> p e g t i", i=4),
+            in_=we_w[:].rearrange("p e (g i t) -> p e g t i", i=4, t=4),
+        )
+        gather_table1(1)
         quantize_weight(1, 0, 4)
         nc.vector.tensor_copy(out=we_sp[:], in_=we_s[:].rearrange("p (m t) -> p t m", t=4))
-        nc.vector.tensor_copy(
-            out=we_wp[:].rearrange("p e t m -> p e m t"), in_=we_w[:].rearrange("p e (m t) -> p e m t", t=4)
-        )
-        gather_table1(0)
+        cast(2, 0, 4, False)
         entity(0)
-        entity(1)
-        gather_table1(1)
         gather_table2(0)
-        quantize_weight(2, 0, 4)
         cast(3, 0, 2, False)
-        cast(3, 2, 4, False)
+        entity(1)
+        quantize_weight(2, 0, 4)
         early = [products(0, 0)]
+        cast(3, 2, 4, True)
         quantize_weight(3, 0, 2)
         quantize_weight(3, 2, 4)
-        early.append(products(1, 0))
-        gather_table2(1)
+        n_w = keep.tile([P, 2, 2 * N], U8, name="n_w", tag="raw3", align_bytes=64)
+        n_s = keep.tile([P, 2, N], U8, name="n_s", tag="raw2", align_bytes=64)
+        nc.gpsimd.memset(n_s[:].rearrange("p a n -> p (a n)").bitcast(I32), 0)
+        for e, (words, scales) in enumerate(((nr_words, nr_scales), (ni_words, ni_scales))):
+            nc.sync.dma_start(out=n_w[:, e, :].bitcast(I32), in_=words[0].bitcast(I32))
+            for q in range(4):
+                nc.sync.dma_start(out=n_s[32 * q : 32 * q + 4, e, :].bitcast(I32), in_=scales[0, 4 * q : 4 * q + 4, :].bitcast(I32))
 
         pending = []
         for c in range(NCH):
             pr = early[c] if c < len(early) else products(c, 0)
             pi = products(c, 1)
+            if c == 0:
+                gather_table2(1)
             if c + 2 < NCH:
                 entity(c + 2)
             pending.append((c, combine(c, pr, pi)))

@@ -23,7 +23,7 @@ CH = 128
 NCH = J // CH
 HALF = J // 2
 LAG = 2
-VECTOR_ADD_CHUNKS = 1
+KINDS = "GGGGGGGV"
 
 
 def tile_list_ckg_sig_kernel(
@@ -65,22 +65,24 @@ def tile_list_ckg_sig_kernel(
             nc.sync.dma_start(out=dst[first : first + count, :].bitcast(I32), in_=rows.bitcast(I32))
 
         nc.sync.dma_start(list1[:], offs)
+        load_words(we_w[:, 0, :], wer_words)
+        for q in range(4):
+            load_rows(tab_s, 32 * q, 4, tab_scales[0, 4 * q : 4 * q + 4, :])
         nc.sync.dma_start(list2[:], offs2)
         load_weight(0)
         for q in range(4):
-            load_rows(tab_s, 32 * q, 4, tab_scales[0, 4 * q : 4 * q + 4, :])
-        load_weight(1)
-        for q in range(4):
             load_rows(tab2_s, 32 * q, 8, tab2_scales[:, 4 * q : 4 * q + 4, :])
         load_words(tab_w[:].bitcast(I32), tab_words)
-        for q in range(4):
-            load_rows(we_s, 32 * q, 4, wer_scales[0, 4 * q : 4 * q + 4, :])
-        load_words(we_w[:, 0, :], wer_words)
         load_words(we_w[:, 1, :], wei_words)
-        load_weight(2)
+        for q in range(2):
+            load_rows(we_s, 32 * q, 4, wer_scales[0, 4 * q : 4 * q + 4, :])
+        load_weight(1)
+        for q in range(2, 4):
+            load_rows(we_s, 32 * q, 4, wer_scales[0, 4 * q : 4 * q + 4, :])
         for q in range(4):
             load_rows(we_s, 32 * q + 4, 4, wei_scales[0, 4 * q : 4 * q + 4, :])
         load_words(tab2_w[:].bitcast(I32), tab2_words)
+        load_weight(2)
         load_weight(3)
 
         v_s = kept([P, J], U8, "v_s")
@@ -92,7 +94,7 @@ def tile_list_ckg_sig_kernel(
         we_sp = kept([P, 4, P], U8, "we_sp")
         hc = HALF // 16
 
-        grouped = [kept([P, 4, P, 4], BF16, f"grouped{i}") for i in range(4)]
+        grouped = [keep.tile([P, 4, P, 4], BF16, name=f"grouped{i}", tag=f"grouped{i}", align_bytes=64) for i in range(4)]
         wr_w = [kept([P, 4, P], U32, f"wr_w{i}") for i in range(4)]
         wr_s = [kept([P, 4, P], U8, f"wr_s{i}") for i in range(4)]
 
@@ -121,7 +123,7 @@ def tile_list_ckg_sig_kernel(
 
         def entity(c):
             h, c0 = divmod(c * CH, HALF)
-            ae[c] = ring.tile([P, 2, CH, 4], F32, name="ae", bufs=2)
+            ae[c] = ring.tile([P, 2, CH // 2, 4, 2], F32, name="ae", bufs=2)
             for e in range(2):
                 bank = psum.tile([P, 4, CH], F32, name="ae_bank")
                 for t in range(4):
@@ -134,11 +136,12 @@ def tile_list_ckg_sig_kernel(
                         start=True,
                         stop=True,
                     )
-                nc.scalar.copy(out=ae[c][:, e, :, :], in_=bank[:].rearrange("p t j -> p j t"))
+                nc.scalar.copy(out=ae[c][:, e], in_=bank[:].rearrange("p t (g i) -> p g t i", i=2))
 
         def products(c, e):
             h, c0 = divmod(c * CH, HALF)
             bank = psum.tile([P, 4, CH], F32, name=f"ar_bank{e}")
+            prod = ring.tile([P, 2, CH // 2, 4, 2], F32, name=f"prod{e}")
             for t in range(4):
                 for a in range(2):
                     nc.tensor.matmul_mx(
@@ -150,20 +153,20 @@ def tile_list_ckg_sig_kernel(
                         start=(a == 0),
                         stop=(a == 1),
                     )
-            prod = ring.tile([P, 2, CH, 4], F32, name=f"prod{e}")
-            nc.vector.tensor_tensor(
-                out=prod[:],
-                in0=bank[:].rearrange("p t j -> p j t").unsqueeze(1).to_broadcast([P, 2, CH, 4]),
-                in1=ae[c][:],
-                op=MULT,
-            )
+            for x in range(2):
+                nc.vector.tensor_tensor(out=prod[:, x], in0=bank[:].rearrange("p t (g i) -> p g t i", i=2), in1=ae[c][:, x], op=MULT)
             return prod
 
         def combine(c, pr, pi):
-            eng = nc.vector if c >= NCH - VECTOR_ADD_CHUNKS else nc.gpsimd
             hb = ring.tile([P, 2, CH, 4], BF16, name="hb", align_bytes=64)
-            eng.tensor_tensor(out=hb[:, 0], in0=pr[:, 0], in1=pi[:, 1], op=SUB)
-            eng.tensor_tensor(out=hb[:, 1], in0=pr[:, 1], in1=pi[:, 0], op=ADD)
+            eng = nc.vector if KINDS[c] == "V" else nc.gpsimd
+            for e, op in enumerate((SUB, ADD)):
+                eng.tensor_tensor(
+                    out=hb[:, e].rearrange("p (g i) t -> p g i t", i=2),
+                    in0=pr[:, e].rearrange("p g t i -> p g i t"),
+                    in1=pi[:, 1 - e].rearrange("p g t i -> p g i t"),
+                    op=op,
+                )
             return hb
 
         out_v = out.rearrange("(g p) j -> p g j", p=P)
@@ -200,25 +203,26 @@ def tile_list_ckg_sig_kernel(
         nc.vector.tensor_copy(v2_s0[:], tab2_s[:].indirect(list2[:]))
         cast(0, 0, 4, False)
         cast(1, 0, 4, False)
-        v2_s1 = keep.tile([P, J], U8, name="v2_s1", tag="raw1", align_bytes=64)
+        v2_s1 = keep.tile([P, J], U8, name="v2_s1", tag="raw0", align_bytes=64)
         nc.gpsimd.memset(v2_s1[96:128, :].bitcast(I32), 0)
         nc.sync.dma_start(out=v2_s1[0:100, :].bitcast(I32), in_=v2_s0[4:104, :].bitcast(I32))
-        quantize_weight(0, 0, 4)
         gather_table1(0)
         nc.vector.tensor_copy(
             out=we_wp[:].rearrange("p e t (g i) -> p e g t i", i=4),
             in_=we_w[:].rearrange("p e (g i t) -> p e g t i", i=4, t=4),
         )
-        gather_table1(1)
-        quantize_weight(1, 0, 4)
         nc.vector.tensor_copy(out=we_sp[:], in_=we_s[:].rearrange("p (m t) -> p t m", t=4))
-        cast(2, 0, 4, False)
+        gather_table1(1)
+        quantize_weight(0, 0, 4)
         entity(0)
         gather_table2(0)
+        quantize_weight(1, 0, 4)
+        cast(2, 0, 4, False)
         cast(3, 0, 2, False)
         entity(1)
-        quantize_weight(2, 0, 4)
         early = [products(0, 0)]
+        gather_table2(1)
+        quantize_weight(2, 0, 4)
         cast(3, 2, 4, True)
         quantize_weight(3, 0, 2)
         quantize_weight(3, 2, 4)
@@ -234,8 +238,6 @@ def tile_list_ckg_sig_kernel(
         for c in range(NCH):
             pr = early[c] if c < len(early) else products(c, 0)
             pi = products(c, 1)
-            if c == 0:
-                gather_table2(1)
             if c + 2 < NCH:
                 entity(c + 2)
             pending.append((c, combine(c, pr, pi)))

@@ -123,7 +123,7 @@ def tile_list_ckg_sig_kernel(
 
         def entity(c):
             h, c0 = divmod(c * CH, HALF)
-            ae[c] = ring.tile([P, 2, CH // 2, 4, 2], F32, name="ae", bufs=2)
+            ae[c] = ring.tile([P, 2, CH, 4], F32, name="ae", bufs=2)
             for e in range(2):
                 bank = psum.tile([P, 4, CH], F32, name="ae_bank")
                 for t in range(4):
@@ -136,12 +136,12 @@ def tile_list_ckg_sig_kernel(
                         start=True,
                         stop=True,
                     )
-                nc.scalar.copy(out=ae[c][:, e], in_=bank[:].rearrange("p t (g i) -> p g t i", i=2))
+                nc.scalar.copy(out=ae[c][:, e], in_=bank[:].rearrange("p t j -> p j t"))
 
         def products(c, e):
             h, c0 = divmod(c * CH, HALF)
             bank = psum.tile([P, 4, CH], F32, name=f"ar_bank{e}")
-            prod = ring.tile([P, 2, CH // 2, 4, 2], F32, name=f"prod{e}")
+            prod = ring.tile([P, 2, CH, 4], F32, name=f"prod{e}")
             for t in range(4):
                 for a in range(2):
                     nc.tensor.matmul_mx(
@@ -153,20 +153,19 @@ def tile_list_ckg_sig_kernel(
                         start=(a == 0),
                         stop=(a == 1),
                     )
-            for x in range(2):
-                nc.vector.tensor_tensor(out=prod[:, x], in0=bank[:].rearrange("p t (g i) -> p g t i", i=2), in1=ae[c][:, x], op=MULT)
+            nc.vector.tensor_tensor(
+                out=prod[:],
+                in0=ae[c][:],
+                in1=bank[:].rearrange("p t j -> p j t").unsqueeze(1).to_broadcast([P, 2, CH, 4]),
+                op=MULT,
+            )
             return prod
 
         def combine(c, pr, pi):
             hb = ring.tile([P, 2, CH, 4], BF16, name="hb", align_bytes=64)
             eng = nc.vector if KINDS[c] == "V" else nc.gpsimd
             for e, op in enumerate((SUB, ADD)):
-                eng.tensor_tensor(
-                    out=hb[:, e].rearrange("p (g i) t -> p g i t", i=2),
-                    in0=pr[:, e].rearrange("p g t i -> p g i t"),
-                    in1=pi[:, 1 - e].rearrange("p g t i -> p g i t"),
-                    op=op,
-                )
+                eng.tensor_tensor(out=hb[:, e], in0=pr[:, e], in1=pi[:, 1 - e], op=op)
             return hb
 
         out_v = out.rearrange("(g p) j -> p g j", p=P)
@@ -218,14 +217,12 @@ def tile_list_ckg_sig_kernel(
         gather_table2(0)
         quantize_weight(1, 0, 4)
         cast(2, 0, 4, False)
-        cast(3, 0, 2, False)
         entity(1)
+        cast(3, 0, 4, True)
         early = [products(0, 0)]
-        gather_table2(1)
+        quantize_weight(3, 0, 4)
         quantize_weight(2, 0, 4)
-        cast(3, 2, 4, True)
-        quantize_weight(3, 0, 2)
-        quantize_weight(3, 2, 4)
+        gather_table2(1)
         n_w = keep.tile([P, 2, 2 * N], U8, name="n_w", tag="raw3", align_bytes=64)
         n_s = keep.tile([P, 2, N], U8, name="n_s", tag="raw2", align_bytes=64)
         nc.gpsimd.memset(n_s[:].rearrange("p a n -> p (a n)").bitcast(I32), 0)

@@ -22,8 +22,6 @@ P = 128
 CH = 128
 NCH = J // CH
 HALF = J // 2
-LAG = 2
-KINDS = "GGGGGGGV"
 
 
 def tile_list_ckg_sig_kernel(
@@ -161,12 +159,8 @@ def tile_list_ckg_sig_kernel(
             )
             return prod
 
-        def combine(c, pr, pi):
-            hb = ring.tile([P, 2, CH, 4], BF16, name="hb", align_bytes=64)
-            eng = nc.vector if KINDS[c] == "V" else nc.gpsimd
-            for e, op in enumerate((SUB, ADD)):
-                eng.tensor_tensor(out=hb[:, e], in0=pr[:, e], in1=pi[:, 1 - e], op=op)
-            return hb
+        def combine(eng, hb, pr, pi, e, j0, j1):
+            eng.tensor_tensor(out=hb[:, e, j0:j1], in0=pr[:, e, j0:j1], in1=pi[:, 1 - e, j0:j1], op=(SUB, ADD)[e])
 
         out_v = out.rearrange("(g p) j -> p g j", p=P)
 
@@ -202,7 +196,7 @@ def tile_list_ckg_sig_kernel(
         nc.vector.tensor_copy(v2_s0[:], tab2_s[:].indirect(list2[:]))
         cast(0, 0, 4, False)
         cast(1, 0, 4, False)
-        v2_s1 = keep.tile([P, J], U8, name="v2_s1", tag="raw0", align_bytes=64)
+        v2_s1 = keep.tile([P, J], U8, name="v2_s1", tag="raw1", align_bytes=64)
         nc.gpsimd.memset(v2_s1[96:128, :].bitcast(I32), 0)
         nc.sync.dma_start(out=v2_s1[0:100, :].bitcast(I32), in_=v2_s0[4:104, :].bitcast(I32))
         gather_table1(0)
@@ -217,12 +211,14 @@ def tile_list_ckg_sig_kernel(
         gather_table2(0)
         quantize_weight(1, 0, 4)
         cast(2, 0, 4, False)
+        cast(3, 0, 2, False)
         entity(1)
-        cast(3, 0, 4, True)
         early = [products(0, 0)]
-        quantize_weight(3, 0, 4)
-        quantize_weight(2, 0, 4)
         gather_table2(1)
+        quantize_weight(2, 0, 4)
+        cast(3, 2, 4, True)
+        quantize_weight(3, 2, 4)
+        quantize_weight(3, 0, 2)
         n_w = keep.tile([P, 2, 2 * N], U8, name="n_w", tag="raw3", align_bytes=64)
         n_s = keep.tile([P, 2, N], U8, name="n_s", tag="raw2", align_bytes=64)
         nc.gpsimd.memset(n_s[:].rearrange("p a n -> p (a n)").bitcast(I32), 0)
@@ -231,14 +227,22 @@ def tile_list_ckg_sig_kernel(
             for q in range(4):
                 nc.sync.dma_start(out=n_s[32 * q : 32 * q + 4, e, :].bitcast(I32), in_=scales[0, 4 * q : 4 * q + 4, :].bitcast(I32))
 
-        pending = []
+        terms = {}
         for c in range(NCH):
             pr = early[c] if c < len(early) else products(c, 0)
             pi = products(c, 1)
             if c + 2 < NCH:
                 entity(c + 2)
-            pending.append((c, combine(c, pr, pi)))
-            if len(pending) > LAG:
-                score(*pending.pop(0))
-        for item in pending:
-            score(*item)
+            if c >= 1:
+                combine(nc.vector, *terms[c - 1], 1, CH // 2, CH)
+            if c >= 2:
+                score(c - 2, terms[c - 2][0])
+            terms[c] = (ring.tile([P, 2, CH, 4], BF16, name="hb", bufs=2, align_bytes=64), pr, pi)
+            if c < NCH - 1:
+                combine(nc.gpsimd, *terms[c], 0, 0, CH)
+                combine(nc.gpsimd, *terms[c], 1, 0, CH // 2)
+            else:
+                combine(nc.vector, *terms[c], 0, 0, CH)
+                combine(nc.vector, *terms[c], 1, 0, CH)
+        for c in range(NCH - 2, NCH):
+            score(c, terms[c][0])

@@ -96,9 +96,9 @@ def tile_list_ckg_sig_kernel(
         wr_w = [kept([P, 4, P], U32, f"wr_w{i}") for i in range(4)]
         wr_s = [kept([P, 4, P], U8, f"wr_s{i}") for i in range(4)]
 
-        def cast(i, t0, t1, on_vector):
-            dst = grouped[i][:, t0:t1, :, :].rearrange("p t m j -> p m t j")
-            src = raw[i][:].rearrange("p j (m t) -> p m t j", t=4)[:, :, t0:t1, :]
+        def cast(i, m0, m1, on_vector):
+            dst = grouped[i][:, :, m0:m1, :].rearrange("p t m j -> p m j t")
+            src = raw[i][:].rearrange("p j (m t) -> p m j t", t=4)[:, m0:m1, :, :]
             if on_vector:
                 nc.vector.tensor_copy(out=dst, in_=src)
             else:
@@ -194,8 +194,8 @@ def tile_list_ckg_sig_kernel(
 
         nc.vector.tensor_copy(v_s[:], tab_s[:].indirect(list1[:]))
         nc.vector.tensor_copy(v2_s0[:], tab2_s[:].indirect(list2[:]))
-        cast(0, 0, 4, False)
-        cast(1, 0, 4, False)
+        cast(0, 0, P, False)
+        cast(1, 0, P, False)
         v2_s1 = keep.tile([P, J], U8, name="v2_s1", tag="raw1", align_bytes=64)
         nc.gpsimd.memset(v2_s1[96:128, :].bitcast(I32), 0)
         nc.sync.dma_start(out=v2_s1[0:100, :].bitcast(I32), in_=v2_s0[4:104, :].bitcast(I32))
@@ -210,15 +210,14 @@ def tile_list_ckg_sig_kernel(
         entity(0)
         gather_table2(0)
         quantize_weight(1, 0, 4)
-        cast(2, 0, 4, False)
-        cast(3, 0, 2, False)
+        cast(2, 0, P, False)
+        cast(3, 0, P // 2, False)
         entity(1)
         early = [products(0, 0)]
         gather_table2(1)
         quantize_weight(2, 0, 4)
-        cast(3, 2, 4, True)
-        quantize_weight(3, 2, 4)
-        quantize_weight(3, 0, 2)
+        cast(3, P // 2, P, True)
+        quantize_weight(3, 0, 4)
         n_w = keep.tile([P, 2, 2 * N], U8, name="n_w", tag="raw3", align_bytes=64)
         n_s = keep.tile([P, 2, N], U8, name="n_s", tag="raw2", align_bytes=64)
         nc.gpsimd.memset(n_s[:].rearrange("p a n -> p (a n)").bitcast(I32), 0)

@@ -22,6 +22,8 @@ P = 128
 CH = 128
 NCH = J // CH
 HALF = J // 2
+FIRST = 2 * CH
+G_HI = 96
 
 
 def tile_list_ckg_sig_kernel(
@@ -47,9 +49,11 @@ def tile_list_ckg_sig_kernel(
         we_s = keep.tile([P, R], U8, name="we_s", tag="we_s", align_bytes=64)
         raw = [keep.tile([P, 4, R], F32, name=f"raw{i}", tag=f"raw{i}", align_bytes=64) for i in range(4)]
 
+        v2_s1 = kept([P, J], U8, "v2_s1")
+        nc.gpsimd.memset(tab2_s[:].bitcast(I32), 0)
         nc.vector.memset(tab_s[:].bitcast(I32), 0)
-        nc.vector.memset(tab2_s[:].bitcast(I32), 0)
-        nc.vector.memset(we_s[:].bitcast(I32), 0)
+        nc.gpsimd.memset(we_s[:].bitcast(I32), 0)
+        nc.gpsimd.memset(v2_s1[96:128, :].bitcast(I32), 0)
 
         def load_words(dst, words):
             nc.sync.dma_start(out=dst, in_=words[0].rearrange("p c i -> p (c i)").bitcast(I32))
@@ -62,26 +66,29 @@ def tile_list_ckg_sig_kernel(
         def load_rows(dst, first, count, rows):
             nc.sync.dma_start(out=dst[first : first + count, :].bitcast(I32), in_=rows.bitcast(I32))
 
-        nc.sync.dma_start(list1[:], offs)
-        load_words(we_w[:, 0, :], wer_words)
-        for q in range(4):
-            load_rows(tab_s, 32 * q, 4, tab_scales[0, 4 * q : 4 * q + 4, :])
+        we_rows = [(32 * q + 4 * e, scales[0, 4 * q : 4 * q + 4, :]) for e, scales in enumerate((wer_scales, wei_scales)) for q in range(4)]
+
+        def load_we_rows(i0, i1):
+            for first, rows in we_rows[i0:i1]:
+                load_rows(we_s, first, 4, rows)
+
         nc.sync.dma_start(list2[:], offs2)
-        load_weight(0)
+        nc.sync.dma_start(list1[:], offs)
         for q in range(4):
             load_rows(tab2_s, 32 * q, 8, tab2_scales[:, 4 * q : 4 * q + 4, :])
-        load_words(tab_w[:].bitcast(I32), tab_words)
-        load_words(we_w[:, 1, :], wei_words)
-        for q in range(2):
-            load_rows(we_s, 32 * q, 4, wer_scales[0, 4 * q : 4 * q + 4, :])
-        load_weight(1)
-        for q in range(2, 4):
-            load_rows(we_s, 32 * q, 4, wer_scales[0, 4 * q : 4 * q + 4, :])
-        for q in range(4):
-            load_rows(we_s, 32 * q + 4, 4, wei_scales[0, 4 * q : 4 * q + 4, :])
         load_words(tab2_w[:].bitcast(I32), tab2_words)
+        load_weight(0)
+        for q in range(4):
+            load_rows(tab_s, 32 * q, 4, tab_scales[0, 4 * q : 4 * q + 4, :])
+        load_weight(1)
+        load_we_rows(0, 1)
         load_weight(2)
+        load_words(we_w[:, 0, :], wer_words)
+        load_we_rows(1, 5)
         load_weight(3)
+        load_we_rows(5, 8)
+        load_words(we_w[:, 1, :], wei_words)
+        load_words(tab_w[:].bitcast(I32), tab_words)
 
         v_s = kept([P, J], U8, "v_s")
         v_w = {}
@@ -112,7 +119,7 @@ def tile_list_ckg_sig_kernel(
             )
 
         def gather_table2(h):
-            v2_both[h] = keep.tile([P, HALF], U32, name="v2_both", tag="we_s", align_bytes=64)
+            v2_both[h] = keep.tile([P, HALF], U32, name="v2_both", tag="tab2_s", align_bytes=64)
             v2_w[h] = ring.tile([P, 2, HALF], U16, name="v2_w", bufs=2, align_bytes=64)
             nc.vector.tensor_copy(v2_both[h][:], tab2_w[:].indirect(list2[:, h * hc : (h + 1) * hc]))
             nc.vector.tensor_copy(out=v2_w[h][:], in_=v2_both[h][:].bitcast(U16).rearrange("p (j d) -> p d j", d=2))
@@ -120,7 +127,7 @@ def tile_list_ckg_sig_kernel(
         ae = {}
 
         def entity(c):
-            h, c0 = divmod(c * CH, HALF)
+            h, c0 = (0, c * CH) if c * CH < FIRST else (1, c * CH - FIRST)
             ae[c] = ring.tile([P, 2, CH, 4], F32, name="ae", bufs=2)
             for e in range(2):
                 bank = psum.tile([P, 4, CH], F32, name="ae_bank")
@@ -189,35 +196,27 @@ def tile_list_ckg_sig_kernel(
             nc.sync.dma_start(out=out_v[:, :, c * CH : (c + 1) * CH], in_=res[:])
 
         def gather_table1(h):
-            v_w[h] = ring.tile([P, HALF], U32, name="v_w", bufs=2, align_bytes=64)
-            nc.vector.tensor_copy(v_w[h][:], tab_w[:].indirect(list1[:, h * hc : (h + 1) * hc]))
+            j0, j1 = ((0, FIRST), (FIRST, J))[h]
+            v_w[h] = kept([P, j1 - j0], U32, f"v_w{h}")
+            nc.vector.tensor_copy(v_w[h][:], tab_w[:].indirect(list1[:, j0 // 16 : j1 // 16]))
 
-        nc.vector.tensor_copy(v_s[:], tab_s[:].indirect(list1[:]))
         nc.vector.tensor_copy(v2_s0[:], tab2_s[:].indirect(list2[:]))
-        cast(0, 0, P, False)
-        cast(1, 0, P, False)
-        v2_s1 = keep.tile([P, J], U8, name="v2_s1", tag="raw1", align_bytes=64)
-        nc.gpsimd.memset(v2_s1[96:128, :].bitcast(I32), 0)
         nc.sync.dma_start(out=v2_s1[0:100, :].bitcast(I32), in_=v2_s0[4:104, :].bitcast(I32))
-        gather_table1(0)
+        gather_table2(0)
+        gather_table2(1)
+        nc.vector.tensor_copy(v_s[:], tab_s[:].indirect(list1[:]))
+        for i in range(4):
+            cast(i, 0, P, False)
+            quantize_weight(i, 0, 4)
         nc.vector.tensor_copy(
             out=we_wp[:].rearrange("p e t (g i) -> p e g t i", i=4),
             in_=we_w[:].rearrange("p e (g i t) -> p e g t i", i=4, t=4),
         )
         nc.vector.tensor_copy(out=we_sp[:], in_=we_s[:].rearrange("p (m t) -> p t m", t=4))
-        gather_table1(1)
-        quantize_weight(0, 0, 4)
+        gather_table1(0)
         entity(0)
-        gather_table2(0)
-        quantize_weight(1, 0, 4)
-        cast(2, 0, P, False)
-        cast(3, 0, P // 2, False)
         entity(1)
-        early = [products(0, 0)]
-        gather_table2(1)
-        quantize_weight(2, 0, 4)
-        cast(3, P // 2, P, True)
-        quantize_weight(3, 0, 4)
+        gather_table1(1)
         n_w = keep.tile([P, 2, 2 * N], U8, name="n_w", tag="raw3", align_bytes=64)
         n_s = keep.tile([P, 2, N], U8, name="n_s", tag="raw2", align_bytes=64)
         nc.gpsimd.memset(n_s[:].rearrange("p a n -> p (a n)").bitcast(I32), 0)
@@ -228,18 +227,18 @@ def tile_list_ckg_sig_kernel(
 
         terms = {}
         for c in range(NCH):
-            pr = early[c] if c < len(early) else products(c, 0)
+            pr = products(c, 0)
             pi = products(c, 1)
             if c + 2 < NCH:
                 entity(c + 2)
             if c >= 1:
-                combine(nc.vector, *terms[c - 1], 1, CH // 2, CH)
+                combine(nc.vector, *terms[c - 1], 1, G_HI, CH)
             if c >= 2:
                 score(c - 2, terms[c - 2][0])
             terms[c] = (ring.tile([P, 2, CH, 4], BF16, name="hb", bufs=2, align_bytes=64), pr, pi)
             if c < NCH - 1:
                 combine(nc.gpsimd, *terms[c], 0, 0, CH)
-                combine(nc.gpsimd, *terms[c], 1, 0, CH // 2)
+                combine(nc.gpsimd, *terms[c], 1, 0, G_HI)
             else:
                 combine(nc.vector, *terms[c], 0, 0, CH)
                 combine(nc.vector, *terms[c], 1, 0, CH)

@@ -15,7 +15,7 @@ FP8X4 = mybir.dt.float8_e4m3fn_x4
 FP4X4 = mybir.dt.float4_e2m1fn_x4
 MULT = mybir.AluOpType.mult
 ADD = mybir.AluOpType.add
-SUB = mybir.AluOpType.subtract
+COPY = mybir.ActivationFunctionType.Copy
 SIGMOID = mybir.ActivationFunctionType.Sigmoid
 
 P = 128
@@ -23,7 +23,6 @@ CH = 128
 NCH = J // CH
 HALF = J // 2
 FIRST = 2 * CH
-G_HI = 96
 
 
 def tile_list_ckg_sig_kernel(
@@ -128,7 +127,7 @@ def tile_list_ckg_sig_kernel(
 
         def entity(c):
             h, c0 = (0, c * CH) if c * CH < FIRST else (1, c * CH - FIRST)
-            ae[c] = ring.tile([P, 2, CH, 4], F32, name="ae", bufs=2)
+            ae[c] = ring.tile([P, 3, CH, 4], F32, name="ae", bufs=2)
             for e in range(2):
                 bank = psum.tile([P, 4, CH], F32, name="ae_bank")
                 for t in range(4):
@@ -141,7 +140,8 @@ def tile_list_ckg_sig_kernel(
                         start=True,
                         stop=True,
                     )
-                nc.scalar.copy(out=ae[c][:, e], in_=bank[:].rearrange("p t j -> p j t"))
+                nc.scalar.copy(out=ae[c][:, 1 + e], in_=bank[:].rearrange("p t j -> p j t"))
+            nc.scalar.activation(out=ae[c][:, 0], in_=bank[:].rearrange("p t j -> p j t"), func=COPY, scale=-1.0)
 
         def products(c, e):
             h, c0 = divmod(c * CH, HALF)
@@ -160,14 +160,11 @@ def tile_list_ckg_sig_kernel(
                     )
             nc.vector.tensor_tensor(
                 out=prod[:],
-                in0=ae[c][:],
+                in0=ae[c][:, 1 - e : 3 - e],
                 in1=bank[:].rearrange("p t j -> p j t").unsqueeze(1).to_broadcast([P, 2, CH, 4]),
                 op=MULT,
             )
             return prod
-
-        def combine(eng, hb, pr, pi, e, j0, j1):
-            eng.tensor_tensor(out=hb[:, e, j0:j1], in0=pr[:, e, j0:j1], in1=pi[:, 1 - e, j0:j1], op=(SUB, ADD)[e])
 
         out_v = out.rearrange("(g p) j -> p g j", p=P)
 
@@ -225,22 +222,15 @@ def tile_list_ckg_sig_kernel(
             for q in range(4):
                 nc.sync.dma_start(out=n_s[32 * q : 32 * q + 4, e, :].bitcast(I32), in_=scales[0, 4 * q : 4 * q + 4, :].bitcast(I32))
 
-        terms = {}
+        hb = {}
         for c in range(NCH):
             pr = products(c, 0)
             pi = products(c, 1)
+            if c >= 2:
+                score(c - 2, hb[c - 2])
             if c + 2 < NCH:
                 entity(c + 2)
-            if c >= 1:
-                combine(nc.vector, *terms[c - 1], 1, G_HI, CH)
-            if c >= 2:
-                score(c - 2, terms[c - 2][0])
-            terms[c] = (ring.tile([P, 2, CH, 4], BF16, name="hb", bufs=2, align_bytes=64), pr, pi)
-            if c < NCH - 1:
-                combine(nc.gpsimd, *terms[c], 0, 0, CH)
-                combine(nc.gpsimd, *terms[c], 1, 0, G_HI)
-            else:
-                combine(nc.vector, *terms[c], 0, 0, CH)
-                combine(nc.vector, *terms[c], 1, 0, CH)
+            hb[c] = ring.tile([P, 2, CH, 4], BF16, name="hb", bufs=4, align_bytes=64)
+            (nc.gpsimd if c < NCH - 1 else nc.vector).tensor_tensor(out=hb[c][:], in0=pr[:], in1=pi[:], op=ADD)
         for c in range(NCH - 2, NCH):
-            score(c, terms[c][0])
+            score(c, hb[c])

@@ -44,15 +44,15 @@ def tile_list_ckg_sig_kernel(
         tab_s = kept([P, T], U8, "tab_s")
         tab2_w = kept([P, T], U32, "tab2_w")
         tab2_s = kept([P, T], U8, "tab2_s")
-        we_w = kept([P, 2, R], I32, "we_w")
+        we_w = [kept([P, R], I32, f"we_w{e}") for e in range(2)]
         we_s = keep.tile([P, R], U8, name="we_s", tag="we_s", align_bytes=64)
         raw = [keep.tile([P, 4, R], F32, name=f"raw{i}", tag=f"raw{i}", align_bytes=64) for i in range(4)]
 
         v2_s1 = kept([P, J], U8, "v2_s1")
         nc.gpsimd.memset(tab2_s[:].bitcast(I32), 0)
-        nc.vector.memset(tab_s[:].bitcast(I32), 0)
         nc.gpsimd.memset(we_s[:].bitcast(I32), 0)
-        nc.gpsimd.memset(v2_s1[96:128, :].bitcast(I32), 0)
+        nc.vector.memset(tab_s[:].bitcast(I32), 0)
+        nc.vector.memset(v2_s1[96:128, :].bitcast(I32), 0)
 
         def load_words(dst, words):
             nc.sync.dma_start(out=dst, in_=words[0].rearrange("p c i -> p (c i)").bitcast(I32))
@@ -62,39 +62,40 @@ def tile_list_ckg_sig_kernel(
             a = i % 2
             nc.sync.dma_start(out=raw[i][:], in_=w[512 * a : 512 * (a + 1), :].rearrange("(p j) c -> p j c", j=4))
 
-        def load_rows(dst, first, count, rows):
-            nc.sync.dma_start(out=dst[first : first + count, :].bitcast(I32), in_=rows.bitcast(I32))
+        def load_rows(dst, first, count, rows, eng=nc.sync):
+            eng.dma_start(out=dst[first : first + count, :].bitcast(I32), in_=rows.bitcast(I32))
 
         we_rows = [(32 * q + 4 * e, scales[0, 4 * q : 4 * q + 4, :]) for e, scales in enumerate((wer_scales, wei_scales)) for q in range(4)]
 
-        def load_we_rows(i0, i1):
+        def load_we_rows(i0, i1, eng=nc.sync):
             for first, rows in we_rows[i0:i1]:
-                load_rows(we_s, first, 4, rows)
+                load_rows(we_s, first, 4, rows, eng)
 
-        nc.sync.dma_start(list2[:], offs2)
-        nc.sync.dma_start(list1[:], offs)
-        for q in range(4):
-            load_rows(tab2_s, 32 * q, 8, tab2_scales[:, 4 * q : 4 * q + 4, :])
         load_words(tab2_w[:].bitcast(I32), tab2_words)
+        nc.sync.dma_start(list2[:], offs2)
+        for r in range(4):
+            rows = tab2_scales.rearrange("a (q r) t -> r q a t", r=4)[r]
+            nc.sync.dma_start(out=tab2_s[r:P:16, :].bitcast(I32), in_=rows.bitcast(I32))
+        nc.sync.dma_start(list1[:], offs)
         load_weight(0)
+        load_weight(1)
         for q in range(4):
             load_rows(tab_s, 32 * q, 4, tab_scales[0, 4 * q : 4 * q + 4, :])
-        load_weight(1)
-        load_we_rows(0, 1)
+        load_we_rows(0, 2)
         load_weight(2)
-        load_words(we_w[:, 0, :], wer_words)
-        load_we_rows(1, 5)
         load_weight(3)
-        load_we_rows(5, 8)
-        load_words(we_w[:, 1, :], wei_words)
+        load_words(we_w[0][:], wer_words)
+        load_we_rows(2, 7)
+        load_we_rows(7, 8, nc.gpsimd)
         load_words(tab_w[:].bitcast(I32), tab_words)
+        load_words(we_w[1][:], wei_words)
 
         v_s = kept([P, J], U8, "v_s")
         v_w = {}
         v2_s0 = kept([P, J], U8, "v2_s0")
         v2_both = {}
         v2_w = {}
-        we_wp = kept([P, 2, 4, P], I32, "we_wp")
+        we_wp = [kept([P, 4, P], I32, f"we_wp{e}") for e in range(2)]
         we_sp = kept([P, 4, P], U8, "we_sp")
         hc = HALF // 16
 
@@ -133,7 +134,7 @@ def tile_list_ckg_sig_kernel(
                 for t in range(4):
                     nc.tensor.matmul_mx(
                         out=bank[:, t, :],
-                        lhsT=we_wp[:, e, t, :].bitcast(FP8X4),
+                        lhsT=we_wp[e][:, t, :].bitcast(FP8X4),
                         lhsT_scale=we_sp[4 * e :, t, :],
                         rhs=v_w[h][:, c0 : c0 + CH].bitcast(FP8X4),
                         rhs_scale=v_s[:, c * CH : (c + 1) * CH],
@@ -192,25 +193,29 @@ def tile_list_ckg_sig_kernel(
             nc.scalar.activation(out=res[:], in_=bank[:], func=SIGMOID)
             nc.sync.dma_start(out=out_v[:, :, c * CH : (c + 1) * CH], in_=res[:])
 
+        def reorder_words(e):
+            nc.vector.tensor_copy(
+                out=we_wp[e][:].rearrange("p t (g i) -> p g t i", i=4),
+                in_=we_w[e][:].rearrange("p (g i t) -> p g t i", i=4, t=4),
+            )
+
         def gather_table1(h):
             j0, j1 = ((0, FIRST), (FIRST, J))[h]
-            v_w[h] = kept([P, j1 - j0], U32, f"v_w{h}")
+            v_w[h] = keep.tile([P, j1 - j0], U32, name=f"v_w{h}", tag=("v_w0", "we_w1")[h], align_bytes=64)
             nc.vector.tensor_copy(v_w[h][:], tab_w[:].indirect(list1[:, j0 // 16 : j1 // 16]))
 
         nc.vector.tensor_copy(v2_s0[:], tab2_s[:].indirect(list2[:]))
-        nc.sync.dma_start(out=v2_s1[0:100, :].bitcast(I32), in_=v2_s0[4:104, :].bitcast(I32))
+        nc.sync.dma_start(out=v2_s1[0:112, :].bitcast(I32), in_=v2_s0[16:128, :].bitcast(I32))
         gather_table2(0)
         gather_table2(1)
         nc.vector.tensor_copy(v_s[:], tab_s[:].indirect(list1[:]))
         for i in range(4):
             cast(i, 0, P, False)
             quantize_weight(i, 0, 4)
-        nc.vector.tensor_copy(
-            out=we_wp[:].rearrange("p e t (g i) -> p e g t i", i=4),
-            in_=we_w[:].rearrange("p e (g i t) -> p e g t i", i=4, t=4),
-        )
+        reorder_words(0)
         nc.vector.tensor_copy(out=we_sp[:], in_=we_s[:].rearrange("p (m t) -> p t m", t=4))
         gather_table1(0)
+        reorder_words(1)
         entity(0)
         entity(1)
         gather_table1(1)

@@ -21,8 +21,8 @@ SIGMOID = mybir.ActivationFunctionType.Sigmoid
 P = 128
 CH = 128
 NCH = J // CH
-HALF = J // 2
 FIRST = 2 * CH
+ENTITY_PLANE = 8
 
 
 def tile_list_ckg_sig_kernel(
@@ -44,13 +44,15 @@ def tile_list_ckg_sig_kernel(
         tab_s = kept([P, T], U8, "tab_s")
         tab2_w = kept([P, T], U32, "tab2_w")
         tab2_s = kept([P, T], U8, "tab2_s")
-        we_w = [kept([P, R], I32, f"we_w{e}") for e in range(2)]
         we_s = keep.tile([P, R], U8, name="we_s", tag="we_s", align_bytes=64)
         raw = [keep.tile([P, 4, R], F32, name=f"raw{i}", tag=f"raw{i}", align_bytes=64) for i in range(4)]
 
         v2_s1 = kept([P, J], U8, "v2_s1")
         nc.gpsimd.memset(tab2_s[:].bitcast(I32), 0)
         nc.gpsimd.memset(we_s[:].bitcast(I32), 0)
+        warm = kept([P, 2], F32, "warm")
+        nc.gpsimd.memset(warm[:, 0:1], 0.0)
+        nc.scalar.activation(out=warm[:, 1:2], in_=warm[:, 0:1], func=SIGMOID)
         nc.vector.memset(tab_s[:].bitcast(I32), 0)
         nc.vector.memset(v2_s1[96:128, :].bitcast(I32), 0)
 
@@ -65,39 +67,40 @@ def tile_list_ckg_sig_kernel(
         def load_rows(dst, first, count, rows, eng=nc.sync):
             eng.dma_start(out=dst[first : first + count, :].bitcast(I32), in_=rows.bitcast(I32))
 
-        we_rows = [(32 * q + 4 * e, scales[0, 4 * q : 4 * q + 4, :]) for e, scales in enumerate((wer_scales, wei_scales)) for q in range(4)]
+        we_rows = [(32 * q + ENTITY_PLANE + 4 * e, scales[0, 4 * q : 4 * q + 4, :]) for e, scales in enumerate((wer_scales, wei_scales)) for q in range(4)]
 
         def load_we_rows(i0, i1, eng=nc.sync):
             for first, rows in we_rows[i0:i1]:
                 load_rows(we_s, first, 4, rows, eng)
 
-        load_words(tab2_w[:].bitcast(I32), tab2_words)
+        def load_table2_half(h):
+            cols = slice(h * T // 2, (h + 1) * T // 2)
+            nc.sync.dma_start(out=tab2_w[:, cols].bitcast(I32), in_=tab2_words[0].rearrange("p c i -> p (c i)").bitcast(I32)[:, cols])
+
+        load_table2_half(0)
         nc.sync.dma_start(list2[:], offs2)
         for r in range(4):
             rows = tab2_scales.rearrange("a (q r) t -> r q a t", r=4)[r]
             nc.sync.dma_start(out=tab2_s[r:P:16, :].bitcast(I32), in_=rows.bitcast(I32))
-        nc.sync.dma_start(list1[:], offs)
+        load_table2_half(1)
         load_weight(0)
         load_weight(1)
+        nc.sync.dma_start(list1[:], offs)
         for q in range(4):
-            load_rows(tab_s, 32 * q, 4, tab_scales[0, 4 * q : 4 * q + 4, :])
-        load_we_rows(0, 2)
+            load_rows(tab_s, 32 * q + ENTITY_PLANE, 4, tab_scales[0, 4 * q : 4 * q + 4, :])
         load_weight(2)
         load_weight(3)
-        load_words(we_w[0][:], wer_words)
-        load_we_rows(2, 7)
-        load_we_rows(7, 8, nc.gpsimd)
+        load_we_rows(0, 6)
+        load_we_rows(6, 8, nc.gpsimd)
         load_words(tab_w[:].bitcast(I32), tab_words)
-        load_words(we_w[1][:], wei_words)
 
         v_s = kept([P, J], U8, "v_s")
         v_w = {}
         v2_s0 = kept([P, J], U8, "v2_s0")
-        v2_both = {}
-        v2_w = {}
+        v2_both = kept([P, J], U32, "v2_both")
+        v2_w = kept([P, 2, J], U16, "v2_w")
         we_wp = [kept([P, 4, P], I32, f"we_wp{e}") for e in range(2)]
         we_sp = kept([P, 4, P], U8, "we_sp")
-        hc = HALF // 16
 
         grouped = [keep.tile([P, 4, P, 4], BF16, name=f"grouped{i}", tag=f"grouped{i}", align_bytes=64) for i in range(4)]
         wr_w = [kept([P, 4, P], U32, f"wr_w{i}") for i in range(4)]
@@ -118,12 +121,6 @@ def tile_list_ckg_sig_kernel(
                 in_=grouped[i][:, t0:t1, :, :].rearrange("p t m j -> p (t m j)"),
             )
 
-        def gather_table2(h):
-            v2_both[h] = keep.tile([P, HALF], U32, name="v2_both", tag="tab2_s", align_bytes=64)
-            v2_w[h] = ring.tile([P, 2, HALF], U16, name="v2_w", bufs=2, align_bytes=64)
-            nc.vector.tensor_copy(v2_both[h][:], tab2_w[:].indirect(list2[:, h * hc : (h + 1) * hc]))
-            nc.vector.tensor_copy(out=v2_w[h][:], in_=v2_both[h][:].bitcast(U16).rearrange("p (j d) -> p d j", d=2))
-
         ae = {}
 
         def entity(c):
@@ -135,9 +132,9 @@ def tile_list_ckg_sig_kernel(
                     nc.tensor.matmul_mx(
                         out=bank[:, t, :],
                         lhsT=we_wp[e][:, t, :].bitcast(FP8X4),
-                        lhsT_scale=we_sp[4 * e :, t, :],
+                        lhsT_scale=we_sp[ENTITY_PLANE + 4 * e :, t, :],
                         rhs=v_w[h][:, c0 : c0 + CH].bitcast(FP8X4),
-                        rhs_scale=v_s[:, c * CH : (c + 1) * CH],
+                        rhs_scale=v_s[ENTITY_PLANE:, c * CH : (c + 1) * CH],
                         start=True,
                         stop=True,
                     )
@@ -145,7 +142,6 @@ def tile_list_ckg_sig_kernel(
             nc.scalar.activation(out=ae[c][:, 0], in_=bank[:].rearrange("p t j -> p j t"), func=COPY, scale=-1.0)
 
         def products(c, e):
-            h, c0 = divmod(c * CH, HALF)
             bank = psum.tile([P, 4, CH], F32, name=f"ar_bank{e}")
             prod = ring.tile([P, 2, CH, 4], F32, name=f"prod{e}")
             for t in range(4):
@@ -154,17 +150,19 @@ def tile_list_ckg_sig_kernel(
                         out=bank[:, t, :],
                         lhsT=wr_w[2 * e + a][:, t, :].bitcast(FP8X4),
                         lhsT_scale=wr_s[2 * e + a][:, t, :],
-                        rhs=v2_w[h][:, a, c0 : c0 + CH].bitcast(FP4X4),
+                        rhs=v2_w[:, a, c * CH : (c + 1) * CH].bitcast(FP4X4),
                         rhs_scale=(v2_s0, v2_s1)[a][:, c * CH : (c + 1) * CH],
                         start=(a == 0),
                         stop=(a == 1),
                     )
-            nc.vector.tensor_tensor(
-                out=prod[:],
-                in0=ae[c][:, 1 - e : 3 - e],
-                in1=bank[:].rearrange("p t j -> p j t").unsqueeze(1).to_broadcast([P, 2, CH, 4]),
-                op=MULT,
-            )
+            width = 1 if (c, e) == (0, 0) else 2
+            for o in range(0, 2, width):
+                nc.vector.tensor_tensor(
+                    out=prod[:, o : o + width],
+                    in0=ae[c][:, 1 - e + o : 1 - e + o + width],
+                    in1=bank[:].rearrange("p t j -> p j t").unsqueeze(1).to_broadcast([P, width, CH, 4]),
+                    op=MULT,
+                )
             return prod
 
         out_v = out.rearrange("(g p) j -> p g j", p=P)
@@ -191,7 +189,7 @@ def tile_list_ckg_sig_kernel(
                     )
             res = ring.tile([P, 2, CH], F32, name="res")
             nc.scalar.activation(out=res[:], in_=bank[:], func=SIGMOID)
-            nc.sync.dma_start(out=out_v[:, :, c * CH : (c + 1) * CH], in_=res[:])
+            (nc.scalar if c == NCH - 1 else nc.sync).dma_start(out=out_v[:, :, c * CH : (c + 1) * CH], in_=res[:])
 
         def reorder_words(e):
             nc.vector.tensor_copy(
@@ -201,20 +199,26 @@ def tile_list_ckg_sig_kernel(
 
         def gather_table1(h):
             j0, j1 = ((0, FIRST), (FIRST, J))[h]
-            v_w[h] = keep.tile([P, j1 - j0], U32, name=f"v_w{h}", tag=("v_w0", "we_w1")[h], align_bytes=64)
+            v_w[h] = keep.tile([P, j1 - j0], U32, name=f"v_w{h}", tag=("v_w0", "grouped2")[h], align_bytes=64)
             nc.vector.tensor_copy(v_w[h][:], tab_w[:].indirect(list1[:, j0 // 16 : j1 // 16]))
 
         nc.vector.tensor_copy(v2_s0[:], tab2_s[:].indirect(list2[:]))
         nc.sync.dma_start(out=v2_s1[0:112, :].bitcast(I32), in_=v2_s0[16:128, :].bitcast(I32))
-        gather_table2(0)
-        gather_table2(1)
+        nc.vector.tensor_copy(v2_both[:], tab2_w[:].indirect(list2[:]))
         nc.vector.tensor_copy(v_s[:], tab_s[:].indirect(list1[:]))
-        for i in range(4):
+        nc.vector.tensor_copy(out=v2_w[:], in_=v2_both[:].bitcast(U16).rearrange("p (j d) -> p d j", d=2))
+        for i in range(3):
             cast(i, 0, P, False)
             quantize_weight(i, 0, 4)
-        reorder_words(0)
+        we_w = [keep.tile([P, R], I32, name=f"we_w{e}", tag=("raw2", "grouped2")[e], align_bytes=64) for e in range(2)]
+        load_words(we_w[0][:], wer_words)
+        load_words(we_w[1][:], wei_words)
+        cast(3, 0, P // 2, True)
+        cast(3, P // 2, P, False)
+        quantize_weight(3, 0, 4)
         nc.vector.tensor_copy(out=we_sp[:], in_=we_s[:].rearrange("p (m t) -> p t m", t=4))
         gather_table1(0)
+        reorder_words(0)
         reorder_words(1)
         entity(0)
         entity(1)

@@ -19,10 +19,17 @@ COPY = mybir.ActivationFunctionType.Copy
 SIGMOID = mybir.ActivationFunctionType.Sigmoid
 
 P = 128
-CH = 128
-NCH = J // CH
-FIRST = 2 * CH
-ENTITY_PLANE = 8
+QUAD = 32
+CHUNK = 128
+CHUNKS = J // CHUNK
+LAST = CHUNKS - 1
+FIRST_GATHER = 2 * CHUNK
+AHEAD = 2
+LAG = 2
+SECOND_PASS_ROWS = 16
+ENTITY_ROWS = 8
+ROWS_ON_SYNC = 6
+VECTOR_CAST = P // 2
 
 
 def tile_list_ckg_sig_kernel(
@@ -35,8 +42,8 @@ def tile_list_ckg_sig_kernel(
         ring = ctx.enter_context(tc.tile_pool(name="ring", bufs=3))
         psum = ctx.enter_context(tc.psum_pool(name="psum", bufs=2))
 
-        def kept(shape, dtype, name):
-            return keep.tile(shape, dtype, name=name, align_bytes=64)
+        def kept(shape, dtype, name, tag=None):
+            return keep.tile(shape, dtype, name=name, tag=tag or name, align_bytes=64)
 
         list1 = keep.tile([P, J // 16], U16, name="list1")
         list2 = keep.tile([P, J // 16], U16, name="list2")
@@ -44,97 +51,97 @@ def tile_list_ckg_sig_kernel(
         tab_s = kept([P, T], U8, "tab_s")
         tab2_w = kept([P, T], U32, "tab2_w")
         tab2_s = kept([P, T], U8, "tab2_s")
-        we_s = keep.tile([P, R], U8, name="we_s", tag="we_s", align_bytes=64)
-        raw = [keep.tile([P, 4, R], F32, name=f"raw{i}", tag=f"raw{i}", align_bytes=64) for i in range(4)]
-
+        we_s = kept([P, R], U8, "we_s")
+        raw = [kept([P, 4, R], F32, f"raw{i}") for i in range(4)]
         v2_s1 = kept([P, J], U8, "v2_s1")
+
         nc.gpsimd.memset(tab2_s[:].bitcast(I32), 0)
         nc.gpsimd.memset(we_s[:].bitcast(I32), 0)
-        warm = kept([P, 2], F32, "warm")
-        nc.gpsimd.memset(warm[:, 0:1], 0.0)
-        nc.scalar.activation(out=warm[:, 1:2], in_=warm[:, 0:1], func=SIGMOID)
         nc.vector.memset(tab_s[:].bitcast(I32), 0)
-        nc.vector.memset(v2_s1[96:128, :].bitcast(I32), 0)
+        nc.vector.memset(v2_s1[:].bitcast(I32), 0)
 
-        def load_words(dst, words):
-            nc.sync.dma_start(out=dst, in_=words[0].rearrange("p c i -> p (c i)").bitcast(I32))
+        def as_words(words):
+            return words[0].rearrange("p c i -> p (c i)").bitcast(I32)
 
-        def load_weight(i):
-            w = (wrr, wri)[i // 2]
-            a = i % 2
-            nc.sync.dma_start(out=raw[i][:], in_=w[512 * a : 512 * (a + 1), :].rearrange("(p j) c -> p j c", j=4))
+        def load_float_pass(i):
+            rows = (wrr, wri)[i // 2][512 * (i % 2) : 512 * (i % 2 + 1), :]
+            nc.sync.dma_start(out=raw[i][:], in_=rows.rearrange("(p j) c -> p j c", j=4))
 
-        def load_rows(dst, first, count, rows, eng=nc.sync):
-            eng.dma_start(out=dst[first : first + count, :].bitcast(I32), in_=rows.bitcast(I32))
-
-        we_rows = [(32 * q + ENTITY_PLANE + 4 * e, scales[0, 4 * q : 4 * q + 4, :]) for e, scales in enumerate((wer_scales, wei_scales)) for q in range(4)]
-
-        def load_we_rows(i0, i1, eng=nc.sync):
-            for first, rows in we_rows[i0:i1]:
-                load_rows(we_s, first, 4, rows, eng)
+        def load_scale_rows(queue, dst, first, rows):
+            queue.dma_start(out=dst[first : first + 4].bitcast(I32), in_=rows.bitcast(I32))
 
         def load_table2_half(h):
             cols = slice(h * T // 2, (h + 1) * T // 2)
-            nc.sync.dma_start(out=tab2_w[:, cols].bitcast(I32), in_=tab2_words[0].rearrange("p c i -> p (c i)").bitcast(I32)[:, cols])
+            nc.sync.dma_start(out=tab2_w[:, cols].bitcast(I32), in_=as_words(tab2_words)[:, cols])
 
         load_table2_half(0)
         nc.sync.dma_start(list2[:], offs2)
         for r in range(4):
             rows = tab2_scales.rearrange("a (q r) t -> r q a t", r=4)[r]
-            nc.sync.dma_start(out=tab2_s[r:P:16, :].bitcast(I32), in_=rows.bitcast(I32))
+            nc.sync.dma_start(out=tab2_s[r:P:SECOND_PASS_ROWS, :].bitcast(I32), in_=rows.bitcast(I32))
         load_table2_half(1)
-        load_weight(0)
-        load_weight(1)
+        load_float_pass(0)
+        load_float_pass(1)
         nc.sync.dma_start(list1[:], offs)
         for q in range(4):
-            load_rows(tab_s, 32 * q + ENTITY_PLANE, 4, tab_scales[0, 4 * q : 4 * q + 4, :])
-        load_weight(2)
-        load_weight(3)
-        load_we_rows(0, 6)
-        load_we_rows(6, 8, nc.gpsimd)
-        load_words(tab_w[:].bitcast(I32), tab_words)
+            load_scale_rows(nc.sync, tab_s, QUAD * q + ENTITY_ROWS, tab_scales[0, 4 * q : 4 * q + 4, :])
+        load_float_pass(2)
+        load_float_pass(3)
+        for n in range(8):
+            e, q = divmod(n, 4)
+            queue = nc.sync if n < ROWS_ON_SYNC else nc.gpsimd
+            load_scale_rows(queue, we_s, QUAD * q + ENTITY_ROWS + 4 * e, (wer_scales, wei_scales)[e][0, 4 * q : 4 * q + 4, :])
+        nc.sync.dma_start(out=tab_w[:].bitcast(I32), in_=as_words(tab_words))
 
         v_s = kept([P, J], U8, "v_s")
         v_w = {}
         v2_s0 = kept([P, J], U8, "v2_s0")
         v2_both = kept([P, J], U32, "v2_both")
         v2_w = kept([P, 2, J], U16, "v2_w")
-        we_wp = [kept([P, 4, P], I32, f"we_wp{e}") for e in range(2)]
-        we_sp = kept([P, 4, P], U8, "we_sp")
-
-        grouped = [keep.tile([P, 4, P, 4], BF16, name=f"grouped{i}", tag=f"grouped{i}", align_bytes=64) for i in range(4)]
+        we_dealt_w = [kept([P, 4, P], I32, f"we_dealt_w{e}") for e in range(2)]
+        we_dealt_s = kept([P, 4, P], U8, "we_dealt_s")
+        grouped = [kept([P, 4, P, 4], BF16, f"grouped{i}") for i in range(4)]
         wr_w = [kept([P, 4, P], U32, f"wr_w{i}") for i in range(4)]
         wr_s = [kept([P, 4, P], U8, f"wr_s{i}") for i in range(4)]
 
-        def cast(i, m0, m1, on_vector):
-            dst = grouped[i][:, :, m0:m1, :].rearrange("p t m j -> p m j t")
-            src = raw[i][:].rearrange("p j (m t) -> p m j t", t=4)[:, m0:m1, :, :]
-            if on_vector:
-                nc.vector.tensor_copy(out=dst, in_=src)
-            else:
-                nc.scalar.copy(out=dst, in_=src)
-
-        def quantize_weight(i, t0, t1):
-            nc.vector.quantize_mx(
-                out=wr_w[i][:, t0:t1, :].rearrange("p t m -> p (t m)").bitcast(FP8X4),
-                scales=wr_s[i][:, t0:t1, :].rearrange("p t m -> p (t m)"),
-                in_=grouped[i][:, t0:t1, :, :].rearrange("p t m j -> p (t m j)"),
+        def cast(copy, i, m0, m1):
+            copy(
+                out=grouped[i][:, :, m0:m1, :].rearrange("p t m j -> p m j t"),
+                in_=raw[i][:].rearrange("p j (m t) -> p m j t", t=4)[:, m0:m1, :, :],
             )
+
+        def quantize_weight(i):
+            nc.vector.quantize_mx(
+                out=wr_w[i][:].rearrange("p t m -> p (t m)").bitcast(FP8X4),
+                scales=wr_s[i][:].rearrange("p t m -> p (t m)"),
+                in_=grouped[i][:].rearrange("p t m j -> p (t m j)"),
+            )
+
+        def deal_words(e):
+            nc.vector.tensor_copy(
+                out=we_dealt_w[e][:].rearrange("p t (g i) -> p g t i", i=4),
+                in_=we_w[e][:].rearrange("p (g i t) -> p g t i", i=4, t=4),
+            )
+
+        def gather_table_words(piece, tag):
+            j0, j1 = ((0, FIRST_GATHER), (FIRST_GATHER, J))[piece]
+            v_w[piece] = kept([P, j1 - j0], U32, f"v_w{piece}", tag)
+            nc.vector.tensor_copy(v_w[piece][:], tab_w[:].indirect(list1[:, j0 // 16 : j1 // 16]))
 
         ae = {}
 
         def entity(c):
-            h, c0 = (0, c * CH) if c * CH < FIRST else (1, c * CH - FIRST)
-            ae[c] = ring.tile([P, 3, CH, 4], F32, name="ae", bufs=2)
+            piece, j0 = (0, c * CHUNK) if c * CHUNK < FIRST_GATHER else (1, c * CHUNK - FIRST_GATHER)
+            ae[c] = ring.tile([P, 3, CHUNK, 4], F32, name="ae", bufs=AHEAD)
             for e in range(2):
-                bank = psum.tile([P, 4, CH], F32, name="ae_bank")
+                bank = psum.tile([P, 4, CHUNK], F32, name="ae_bank")
                 for t in range(4):
                     nc.tensor.matmul_mx(
                         out=bank[:, t, :],
-                        lhsT=we_wp[e][:, t, :].bitcast(FP8X4),
-                        lhsT_scale=we_sp[ENTITY_PLANE + 4 * e :, t, :],
-                        rhs=v_w[h][:, c0 : c0 + CH].bitcast(FP8X4),
-                        rhs_scale=v_s[ENTITY_PLANE:, c * CH : (c + 1) * CH],
+                        lhsT=we_dealt_w[e][:, t, :].bitcast(FP8X4),
+                        lhsT_scale=we_dealt_s[ENTITY_ROWS + 4 * e :, t, :],
+                        rhs=v_w[piece][:, j0 : j0 + CHUNK].bitcast(FP8X4),
+                        rhs_scale=v_s[ENTITY_ROWS:, c * CHUNK : (c + 1) * CHUNK],
                         start=True,
                         stop=True,
                     )
@@ -142,16 +149,16 @@ def tile_list_ckg_sig_kernel(
             nc.scalar.activation(out=ae[c][:, 0], in_=bank[:].rearrange("p t j -> p j t"), func=COPY, scale=-1.0)
 
         def products(c, e):
-            bank = psum.tile([P, 4, CH], F32, name=f"ar_bank{e}")
-            prod = ring.tile([P, 2, CH, 4], F32, name=f"prod{e}")
+            bank = psum.tile([P, 4, CHUNK], F32, name=f"ar_bank{e}", tag=f"ar_bank{e}")
+            prod = ring.tile([P, 2, CHUNK, 4], F32, name=f"prod{e}")
             for t in range(4):
                 for a in range(2):
                     nc.tensor.matmul_mx(
                         out=bank[:, t, :],
                         lhsT=wr_w[2 * e + a][:, t, :].bitcast(FP8X4),
                         lhsT_scale=wr_s[2 * e + a][:, t, :],
-                        rhs=v2_w[:, a, c * CH : (c + 1) * CH].bitcast(FP4X4),
-                        rhs_scale=(v2_s0, v2_s1)[a][:, c * CH : (c + 1) * CH],
+                        rhs=v2_w[:, a, c * CHUNK : (c + 1) * CHUNK].bitcast(FP4X4),
+                        rhs_scale=(v2_s0, v2_s1)[a][:, c * CHUNK : (c + 1) * CHUNK],
                         start=(a == 0),
                         stop=(a == 1),
                     )
@@ -160,86 +167,84 @@ def tile_list_ckg_sig_kernel(
                 nc.vector.tensor_tensor(
                     out=prod[:, o : o + width],
                     in0=ae[c][:, 1 - e + o : 1 - e + o + width],
-                    in1=bank[:].rearrange("p t j -> p j t").unsqueeze(1).to_broadcast([P, width, CH, 4]),
+                    in1=bank[:].rearrange("p t j -> p j t").unsqueeze(1).to_broadcast([P, width, CHUNK, 4]),
                     op=MULT,
                 )
             return prod
 
         out_v = out.rearrange("(g p) j -> p g j", p=P)
 
-        def score(c, hb):
-            h_w = ring.tile([P, 2, CH], U32, name="h_w", align_bytes=64)
-            h_s = ring.tile([P, 2, CH], U8, name="h_s", align_bytes=64)
+        def score(c):
+            h_w = ring.tile([P, 2, CHUNK], U32, name="h_w", align_bytes=64)
+            h_s = ring.tile([P, 2, CHUNK], U8, name="h_s", align_bytes=64)
             nc.vector.quantize_mx(
                 out=h_w[:].rearrange("p e j -> p (e j)").bitcast(FP8X4),
                 scales=h_s[:].rearrange("p e j -> p (e j)"),
-                in_=hb[:].rearrange("p e j t -> p (e j t)"),
+                in_=hb[c][:].rearrange("p e j t -> p (e j t)"),
             )
-            bank = psum.tile([P, 2, CH], F32, name="y_bank")
-            for g in range(2):
-                for e in range(2):
-                    nc.tensor.matmul_mx(
-                        out=bank[:, g, :],
-                        lhsT=n_w[:, e, 2 * P * g : 2 * P * (g + 1)].bitcast(FP4X4),
-                        lhsT_scale=n_s[:, e, P * g : P * (g + 1)],
-                        rhs=h_w[:, e, :].bitcast(FP8X4),
-                        rhs_scale=h_s[:, e, :],
-                        start=(e == 0),
-                        stop=(e == 1),
-                    )
-            res = ring.tile([P, 2, CH], F32, name="res")
-            nc.scalar.activation(out=res[:], in_=bank[:], func=SIGMOID)
-            (nc.scalar if c == NCH - 1 else nc.sync).dma_start(out=out_v[:, :, c * CH : (c + 1) * CH], in_=res[:])
-
-        def reorder_words(e):
-            nc.vector.tensor_copy(
-                out=we_wp[e][:].rearrange("p t (g i) -> p g t i", i=4),
-                in_=we_w[e][:].rearrange("p (g i t) -> p g t i", i=4, t=4),
-            )
-
-        def gather_table1(h):
-            j0, j1 = ((0, FIRST), (FIRST, J))[h]
-            v_w[h] = keep.tile([P, j1 - j0], U32, name=f"v_w{h}", tag=("v_w0", "grouped2")[h], align_bytes=64)
-            nc.vector.tensor_copy(v_w[h][:], tab_w[:].indirect(list1[:, j0 // 16 : j1 // 16]))
+            groups = 1 if c == LAST else 2
+            for g0 in range(0, 2, groups):
+                bank = psum.tile([P, groups, CHUNK], F32, name="y_bank", tag="ar_bank0" if c == LAST else "y_bank")
+                for g in range(g0, g0 + groups):
+                    for e in range(2):
+                        nc.tensor.matmul_mx(
+                            out=bank[:, g - g0, :],
+                            lhsT=n_w[:, e, 2 * P * g : 2 * P * (g + 1)].bitcast(FP4X4),
+                            lhsT_scale=n_s[:, e, P * g : P * (g + 1)],
+                            rhs=h_w[:, e, :].bitcast(FP8X4),
+                            rhs_scale=h_s[:, e, :],
+                            start=(e == 0),
+                            stop=(e == 1),
+                        )
+                res = ring.tile([P, groups, CHUNK], F32, name="res", tag="res", bufs=4)
+                nc.scalar.activation(out=res[:], in_=bank[:], func=SIGMOID)
+                queue = nc.scalar if (c, g0) == (LAST, 1) else nc.sync
+                queue.dma_start(out=out_v[:, g0 : g0 + groups, c * CHUNK : (c + 1) * CHUNK], in_=res[:])
 
         nc.vector.tensor_copy(v2_s0[:], tab2_s[:].indirect(list2[:]))
-        nc.sync.dma_start(out=v2_s1[0:112, :].bitcast(I32), in_=v2_s0[16:128, :].bitcast(I32))
+        for q in range(4):
+            first = QUAD * q + SECOND_PASS_ROWS
+            load_scale_rows(nc.sync, v2_s1, QUAD * q, v2_s0[first : first + 4, :])
         nc.vector.tensor_copy(v2_both[:], tab2_w[:].indirect(list2[:]))
         nc.vector.tensor_copy(v_s[:], tab_s[:].indirect(list1[:]))
         nc.vector.tensor_copy(out=v2_w[:], in_=v2_both[:].bitcast(U16).rearrange("p (j d) -> p d j", d=2))
+
         for i in range(3):
-            cast(i, 0, P, False)
-            quantize_weight(i, 0, 4)
-        we_w = [keep.tile([P, R], I32, name=f"we_w{e}", tag=("raw2", "grouped2")[e], align_bytes=64) for e in range(2)]
-        load_words(we_w[0][:], wer_words)
-        load_words(we_w[1][:], wei_words)
-        cast(3, 0, P // 2, True)
-        cast(3, P // 2, P, False)
-        quantize_weight(3, 0, 4)
-        nc.vector.tensor_copy(out=we_sp[:], in_=we_s[:].rearrange("p (m t) -> p t m", t=4))
-        gather_table1(0)
-        reorder_words(0)
-        reorder_words(1)
-        entity(0)
-        entity(1)
-        gather_table1(1)
-        n_w = keep.tile([P, 2, 2 * N], U8, name="n_w", tag="raw3", align_bytes=64)
-        n_s = keep.tile([P, 2, N], U8, name="n_s", tag="raw2", align_bytes=64)
-        nc.gpsimd.memset(n_s[:].rearrange("p a n -> p (a n)").bitcast(I32), 0)
+            cast(nc.scalar.copy, i, 0, P)
+            quantize_weight(i)
+        we_w = [kept([P, R], I32, f"we_w{e}", ("raw2", "grouped2")[e]) for e in range(2)]
+        nc.sync.dma_start(out=we_w[0][:], in_=as_words(wer_words))
+        nc.sync.dma_start(out=we_w[1][:], in_=as_words(wei_words))
+        cast(nc.vector.tensor_copy, 3, 0, VECTOR_CAST)
+        cast(nc.scalar.copy, 3, VECTOR_CAST, P)
+        quantize_weight(3)
+        nc.vector.tensor_copy(out=we_dealt_s[:], in_=we_s[:].rearrange("p (m t) -> p t m", t=4))
+
+        gather_table_words(0, None)
+        deal_words(0)
+        deal_words(1)
+        for c in range(AHEAD):
+            entity(c)
+        gather_table_words(1, "grouped2")
+
+        n_w = kept([P, 2, 2 * N], U8, "n_w", "raw3")
+        n_s = kept([P, 2, N], U8, "n_s", "raw2")
+        nc.gpsimd.memset(n_s[:].rearrange("p e n -> p (e n)").bitcast(I32), 0)
         for e, (words, scales) in enumerate(((nr_words, nr_scales), (ni_words, ni_scales))):
             nc.sync.dma_start(out=n_w[:, e, :].bitcast(I32), in_=words[0].bitcast(I32))
             for q in range(4):
-                nc.sync.dma_start(out=n_s[32 * q : 32 * q + 4, e, :].bitcast(I32), in_=scales[0, 4 * q : 4 * q + 4, :].bitcast(I32))
+                load_scale_rows(nc.sync, n_s[:, e, :], QUAD * q, scales[0, 4 * q : 4 * q + 4, :])
 
         hb = {}
-        for c in range(NCH):
-            pr = products(c, 0)
-            pi = products(c, 1)
-            if c >= 2:
-                score(c - 2, hb[c - 2])
-            if c + 2 < NCH:
-                entity(c + 2)
-            hb[c] = ring.tile([P, 2, CH, 4], BF16, name="hb", bufs=4, align_bytes=64)
-            (nc.gpsimd if c < NCH - 1 else nc.vector).tensor_tensor(out=hb[c][:], in0=pr[:], in1=pi[:], op=ADD)
-        for c in range(NCH - 2, NCH):
-            score(c, hb[c])
+        for c in range(CHUNKS):
+            with_arr = products(c, 0)
+            with_ari = products(c, 1)
+            if c >= LAG:
+                score(c - LAG)
+            if c + AHEAD < CHUNKS:
+                entity(c + AHEAD)
+            hb[c] = ring.tile([P, 2, CHUNK, 4], BF16, name="hb", bufs=LAG + 2, align_bytes=64)
+            adder = nc.vector if c == LAST else nc.gpsimd
+            adder.tensor_tensor(out=hb[c][:], in0=with_arr[:], in1=with_ari[:], op=ADD)
+        for c in range(CHUNKS - LAG, CHUNKS):
+            score(c)

@@ -151,16 +151,16 @@ def tile_list_ckg_sig_kernel(
         def products(c, e):
             bank = psum.tile([P, 4, CHUNK], F32, name=f"ar_bank{e}", tag=f"ar_bank{e}")
             prod = ring.tile([P, 2, CHUNK, 4], F32, name=f"prod{e}")
-            for t in range(4):
-                for a in range(2):
+            for a in range(2):
+                for t in range(4):
                     nc.tensor.matmul_mx(
                         out=bank[:, t, :],
                         lhsT=wr_w[2 * e + a][:, t, :].bitcast(FP8X4),
                         lhsT_scale=wr_s[2 * e + a][:, t, :],
                         rhs=v2_w[:, a, c * CHUNK : (c + 1) * CHUNK].bitcast(FP4X4),
                         rhs_scale=(v2_s0, v2_s1)[a][:, c * CHUNK : (c + 1) * CHUNK],
-                        start=(a == 0),
-                        stop=(a == 1),
+                        start=(a, t) == (0, 0),
+                        stop=(a, t) == (1, 3),
                     )
             width = 1 if (c, e) == (0, 0) else 2
             for o in range(0, 2, width):

@@ -67,8 +67,8 @@ def tile_list_ckg_sig_kernel(
             rows = (wrr, wri)[i // 2][512 * (i % 2) : 512 * (i % 2 + 1), :]
             nc.sync.dma_start(out=raw[i][:], in_=rows.rearrange("(p j) c -> p j c", j=4))
 
-        def load_scale_rows(queue, dst, first, rows):
-            queue.dma_start(out=dst[first : first + 4].bitcast(I32), in_=rows.bitcast(I32))
+        def load_scale_rows(queue, dst, first, r, rows):
+            queue.dma_start(out=dst[first + r : P : QUAD].bitcast(I32), in_=rows[r:16:4].bitcast(I32))
 
         def load_table2_half(h):
             cols = slice(h * T // 2, (h + 1) * T // 2)
@@ -83,22 +83,28 @@ def tile_list_ckg_sig_kernel(
         load_float_pass(0)
         load_float_pass(1)
         nc.sync.dma_start(list1[:], offs)
-        for q in range(4):
-            load_scale_rows(nc.sync, tab_s, QUAD * q + ENTITY_ROWS, tab_scales[0, 4 * q : 4 * q + 4, :])
+        for r in range(4):
+            load_scale_rows(nc.sync, tab_s, ENTITY_ROWS, r, tab_scales[0])
         load_float_pass(2)
         load_float_pass(3)
+        v2_s0 = kept([P, J], U8, "v2_s0")
+        nc.vector.tensor_copy(v2_s0[:], tab2_s[:].indirect(list2[:]))
+        for r in range(4):
+            nc.sync.dma_start(
+                out=v2_s1[r:P:QUAD].bitcast(I32), in_=v2_s0[SECOND_PASS_ROWS + r : P : QUAD].bitcast(I32)
+            )
         for n in range(8):
-            e, q = divmod(n, 4)
+            if n == 2:
+                nc.sync.dma_start(out=tab_w[:].bitcast(I32), in_=as_words(tab_words))
+            e, r = divmod(n, 4)
             queue = nc.sync if n < ROWS_ON_SYNC else nc.gpsimd
-            load_scale_rows(queue, we_s, QUAD * q + ENTITY_ROWS + 4 * e, (wer_scales, wei_scales)[e][0, 4 * q : 4 * q + 4, :])
-        nc.sync.dma_start(out=tab_w[:].bitcast(I32), in_=as_words(tab_words))
+            load_scale_rows(queue, we_s, ENTITY_ROWS + 4 * e, r, (wer_scales, wei_scales)[e][0])
 
         v_s = kept([P, J], U8, "v_s")
         v_w = {}
-        v2_s0 = kept([P, J], U8, "v2_s0")
         v2_both = kept([P, J], U32, "v2_both")
         v2_w = kept([P, 2, J], U16, "v2_w")
-        we_dealt_w = [kept([P, 4, P], I32, f"we_dealt_w{e}") for e in range(2)]
+        we_dealt_w = [kept([P, 4, P], U32, f"we_dealt_w{e}") for e in range(2)]
         we_dealt_s = kept([P, 4, P], U8, "we_dealt_s")
         grouped = [kept([P, 4, P, 4], BF16, f"grouped{i}") for i in range(4)]
         wr_w = [kept([P, 4, P], U32, f"wr_w{i}") for i in range(4)]
@@ -118,9 +124,9 @@ def tile_list_ckg_sig_kernel(
             )
 
         def deal_words(e):
-            nc.vector.tensor_copy(
+            nc.scalar.copy(
                 out=we_dealt_w[e][:].rearrange("p t (g i) -> p g t i", i=4),
-                in_=we_w[e][:].rearrange("p (g i t) -> p g t i", i=4, t=4),
+                in_=we_w[e][:].bitcast(U32).rearrange("p (g i t) -> p g t i", i=4, t=4),
             )
 
         def gather_table_words(piece, tag):
@@ -148,9 +154,8 @@ def tile_list_ckg_sig_kernel(
                 nc.scalar.copy(out=ae[c][:, 1 + e], in_=bank[:].rearrange("p t j -> p j t"))
             nc.scalar.activation(out=ae[c][:, 0], in_=bank[:].rearrange("p t j -> p j t"), func=COPY, scale=-1.0)
 
-        def products(c, e):
+        def relation(c, e):
             bank = psum.tile([P, 4, CHUNK], F32, name=f"ar_bank{e}", tag=f"ar_bank{e}")
-            prod = ring.tile([P, 2, CHUNK, 4], F32, name=f"prod{e}")
             for a in range(2):
                 for t in range(4):
                     nc.tensor.matmul_mx(
@@ -162,15 +167,20 @@ def tile_list_ckg_sig_kernel(
                         start=(a, t) == (0, 0),
                         stop=(a, t) == (1, 3),
                     )
-            width = 1 if (c, e) == (0, 0) else 2
-            for o in range(0, 2, width):
+            return bank[:].rearrange("p t j -> p j t").unsqueeze(1)
+
+        def products(c):
+            banks = [relation(c, e) for e in range(2)]
+            prods = [ring.tile([P, 2, CHUNK, 4], F32, name=f"prod{e}") for e in range(2)]
+            steps = ((0, 0, 1), (1, 1, 1), (0, 1, 1), (1, 0, 1)) if c == 0 else ((0, 0, 2), (1, 0, 2))
+            for e, o, width in steps:
                 nc.vector.tensor_tensor(
-                    out=prod[:, o : o + width],
+                    out=prods[e][:, o : o + width],
                     in0=ae[c][:, 1 - e + o : 1 - e + o + width],
-                    in1=bank[:].rearrange("p t j -> p j t").unsqueeze(1).to_broadcast([P, width, CHUNK, 4]),
+                    in1=banks[e].to_broadcast([P, width, CHUNK, 4]),
                     op=MULT,
                 )
-            return prod
+            return prods
 
         out_v = out.rearrange("(g p) j -> p g j", p=P)
 
@@ -201,10 +211,6 @@ def tile_list_ckg_sig_kernel(
                 queue = nc.scalar if (c, g0) == (LAST, 1) else nc.sync
                 queue.dma_start(out=out_v[:, g0 : g0 + groups, c * CHUNK : (c + 1) * CHUNK], in_=res[:])
 
-        nc.vector.tensor_copy(v2_s0[:], tab2_s[:].indirect(list2[:]))
-        for q in range(4):
-            first = QUAD * q + SECOND_PASS_ROWS
-            load_scale_rows(nc.sync, v2_s1, QUAD * q, v2_s0[first : first + 4, :])
         nc.vector.tensor_copy(v2_both[:], tab2_w[:].indirect(list2[:]))
         nc.vector.tensor_copy(v_s[:], tab_s[:].indirect(list1[:]))
         nc.vector.tensor_copy(out=v2_w[:], in_=v2_both[:].bitcast(U16).rearrange("p (j d) -> p d j", d=2))
@@ -225,26 +231,26 @@ def tile_list_ckg_sig_kernel(
         deal_words(1)
         for c in range(AHEAD):
             entity(c)
-        gather_table_words(1, "grouped2")
+        gather_table_words(1, "we_s")
 
         n_w = kept([P, 2, 2 * N], U8, "n_w", "raw3")
         n_s = kept([P, 2, N], U8, "n_s", "raw2")
         nc.gpsimd.memset(n_s[:].rearrange("p e n -> p (e n)").bitcast(I32), 0)
         for e, (words, scales) in enumerate(((nr_words, nr_scales), (ni_words, ni_scales))):
             nc.sync.dma_start(out=n_w[:, e, :].bitcast(I32), in_=words[0].bitcast(I32))
-            for q in range(4):
-                load_scale_rows(nc.sync, n_s[:, e, :], QUAD * q, scales[0, 4 * q : 4 * q + 4, :])
+            for r in range(4):
+                load_scale_rows(nc.sync, n_s[:, e, :], 0, r, scales[0])
 
         hb = {}
         for c in range(CHUNKS):
-            with_arr = products(c, 0)
-            with_ari = products(c, 1)
+            with_arr, with_ari = products(c)
             if c >= LAG:
                 score(c - LAG)
             if c + AHEAD < CHUNKS:
                 entity(c + AHEAD)
             hb[c] = ring.tile([P, 2, CHUNK, 4], BF16, name="hb", bufs=LAG + 2, align_bytes=64)
             adder = nc.vector if c == LAST else nc.gpsimd
-            adder.tensor_tensor(out=hb[c][:], in0=with_arr[:], in1=with_ari[:], op=ADD)
+            for part in (slice(1, 2), slice(0, 1)) if c == 0 else (slice(0, 2),):
+                adder.tensor_tensor(out=hb[c][:, part], in0=with_arr[:, part], in1=with_ari[:, part], op=ADD)
         for c in range(CHUNKS - LAG, CHUNKS):
             score(c)

@@ -187,25 +187,32 @@ def tile_list_ckg_sig_kernel(
         def score(c):
             h_w = ring.tile([P, 2, CHUNK], U32, name="h_w", align_bytes=64)
             h_s = ring.tile([P, 2, CHUNK], U8, name="h_s", align_bytes=64)
-            nc.vector.quantize_mx(
-                out=h_w[:].rearrange("p e j -> p (e j)").bitcast(FP8X4),
-                scales=h_s[:].rearrange("p e j -> p (e j)"),
-                in_=hb[c][:].rearrange("p e j t -> p (e j t)"),
-            )
-            groups = 1 if c == LAST else 2
-            for g0 in range(0, 2, groups):
-                bank = psum.tile([P, groups, CHUNK], F32, name="y_bank", tag="ar_bank0" if c == LAST else "y_bank")
-                for g in range(g0, g0 + groups):
-                    for e in range(2):
-                        nc.tensor.matmul_mx(
-                            out=bank[:, g - g0, :],
-                            lhsT=n_w[:, e, 2 * P * g : 2 * P * (g + 1)].bitcast(FP4X4),
-                            lhsT_scale=n_s[:, e, P * g : P * (g + 1)],
-                            rhs=h_w[:, e, :].bitcast(FP8X4),
-                            rhs_scale=h_s[:, e, :],
-                            start=(e == 0),
-                            stop=(e == 1),
-                        )
+            for part in (slice(0, 1), slice(1, 2)) if c == LAST else (slice(0, 2),):
+                nc.vector.quantize_mx(
+                    out=h_w[:, part].rearrange("p e j -> p (e j)").bitcast(FP8X4),
+                    scales=h_s[:, part].rearrange("p e j -> p (e j)"),
+                    in_=hb[c][:, part].rearrange("p e j t -> p (e j t)"),
+                )
+            if c == LAST:
+                banks = [psum.tile([P, 1, CHUNK], F32, name="y_last", tag="ar_bank0") for g in range(2)]
+                sums = [bank[:, 0, :] for bank in banks]
+                order = [(g, e) for e in range(2) for g in range(2)]
+            else:
+                banks = [psum.tile([P, 2, CHUNK], F32, name="y_bank")]
+                sums = [banks[0][:, g, :] for g in range(2)]
+                order = [(g, e) for g in range(2) for e in range(2)]
+            for g, e in order:
+                nc.tensor.matmul_mx(
+                    out=sums[g],
+                    lhsT=n_w[:, e, 2 * P * g : 2 * P * (g + 1)].bitcast(FP4X4),
+                    lhsT_scale=n_s[:, e, P * g : P * (g + 1)],
+                    rhs=h_w[:, e, :].bitcast(FP8X4),
+                    rhs_scale=h_s[:, e, :],
+                    start=(e == 0),
+                    stop=(e == 1),
+                )
+            groups = 2 // len(banks)
+            for g0, bank in enumerate(banks):
                 res = ring.tile([P, groups, CHUNK], F32, name="res", tag="res", bufs=4)
                 nc.scalar.activation(out=res[:], in_=bank[:], func=SIGMOID)
                 queue = nc.scalar if (c, g0) == (LAST, 1) else nc.sync
@@ -218,7 +225,7 @@ def tile_list_ckg_sig_kernel(
         for i in range(3):
             cast(nc.scalar.copy, i, 0, P)
             quantize_weight(i)
-        we_w = [kept([P, R], I32, f"we_w{e}", ("raw2", "grouped2")[e]) for e in range(2)]
+        we_w = [kept([P, R], I32, f"we_w{e}", ("raw1", "grouped1")[e]) for e in range(2)]
         nc.sync.dma_start(out=we_w[0][:], in_=as_words(wer_words))
         nc.sync.dma_start(out=we_w[1][:], in_=as_words(wei_words))
         cast(nc.vector.tensor_copy, 3, 0, VECTOR_CAST)
@@ -234,7 +241,7 @@ def tile_list_ckg_sig_kernel(
         gather_table_words(1, "we_s")
 
         n_w = kept([P, 2, 2 * N], U8, "n_w", "raw3")
-        n_s = kept([P, 2, N], U8, "n_s", "raw2")
+        n_s = kept([P, 2, N], U8, "n_s", "raw1")
         nc.gpsimd.memset(n_s[:].rearrange("p e n -> p (e n)").bitcast(I32), 0)
         for e, (words, scales) in enumerate(((nr_words, nr_scales), (ni_words, ni_scales))):
             nc.sync.dma_start(out=n_w[:, e, :].bitcast(I32), in_=words[0].bitcast(I32))
@@ -246,11 +253,15 @@ def tile_list_ckg_sig_kernel(
             with_arr, with_ari = products(c)
             if c >= LAG:
                 score(c - LAG)
+            if c == LAST:
+                score(c - 1)
             if c + AHEAD < CHUNKS:
                 entity(c + AHEAD)
-            hb[c] = ring.tile([P, 2, CHUNK, 4], BF16, name="hb", bufs=LAG + 2, align_bytes=64)
+            if c < LAST - 1:
+                hb[c] = ring.tile([P, 2, CHUNK, 4], BF16, name="hb", bufs=LAG + 2, align_bytes=64)
+            else:
+                hb[c] = kept([P, 2, CHUNK, 4], BF16, f"hb{c}", "hb_end")
             adder = nc.vector if c == LAST else nc.gpsimd
-            for part in (slice(1, 2), slice(0, 1)) if c == 0 else (slice(0, 2),):
+            for part in (slice(1, 2), slice(0, 1)) if c == 0 else (slice(0, 1), slice(1, 2)) if c == LAST else (slice(0, 2),):
                 adder.tensor_tensor(out=hb[c][:, part], in0=with_arr[:, part], in1=with_ari[:, part], op=ADD)
-        for c in range(CHUNKS - LAG, CHUNKS):
-            score(c)
+        score(LAST)

@@ -28,7 +28,7 @@ AHEAD = 2
 LAG = 2
 SECOND_PASS_ROWS = 16
 ENTITY_ROWS = 8
-ROWS_ON_SYNC = 6
+ROWS_ON_SYNC = 2
 VECTOR_CAST = P // 2
 
 
@@ -140,7 +140,7 @@ def tile_list_ckg_sig_kernel(
             piece, j0 = (0, c * CHUNK) if c * CHUNK < FIRST_GATHER else (1, c * CHUNK - FIRST_GATHER)
             ae[c] = ring.tile([P, 3, CHUNK, 4], F32, name="ae", bufs=AHEAD)
             for e in range(2):
-                bank = psum.tile([P, 4, CHUNK], F32, name="ae_bank")
+                bank = psum.tile([P, 4, CHUNK], F32, name="ae_bank", bufs=3)
                 for t in range(4):
                     nc.tensor.matmul_mx(
                         out=bank[:, t, :],
@@ -198,7 +198,8 @@ def tile_list_ckg_sig_kernel(
                 sums = [bank[:, 0, :] for bank in banks]
                 order = [(g, e) for e in range(2) for g in range(2)]
             else:
-                banks = [psum.tile([P, 2, CHUNK], F32, name="y_bank")]
+                tag, bufs = ("ar_bank1", 2) if c == LAST - 1 else ("y_bank", 1)
+                banks = [psum.tile([P, 2, CHUNK], F32, name="y_bank", tag=tag, bufs=bufs)]
                 sums = [banks[0][:, g, :] for g in range(2)]
                 order = [(g, e) for g in range(2) for e in range(2)]
             for g, e in order:

@@ -223,9 +223,12 @@ def tile_list_ckg_sig_kernel(
         nc.vector.tensor_copy(v_s[:], tab_s[:].indirect(list1[:]))
         nc.vector.tensor_copy(out=v2_w[:], in_=v2_both[:].bitcast(U16).rearrange("p (j d) -> p d j", d=2))
 
-        for i in range(3):
+        for i in range(2):
             cast(nc.scalar.copy, i, 0, P)
             quantize_weight(i)
+        cast(nc.vector.tensor_copy, 2, 0, VECTOR_CAST)
+        cast(nc.scalar.copy, 2, VECTOR_CAST, P)
+        quantize_weight(2)
         we_w = [kept([P, R], I32, f"we_w{e}", ("raw1", "grouped1")[e]) for e in range(2)]
         nc.sync.dma_start(out=we_w[0][:], in_=as_words(wer_words))
         nc.sync.dma_start(out=we_w[1][:], in_=as_words(wei_words))

@@ -1,6 +1,7 @@
 from contextlib import ExitStack
 
 import concourse.mybir as mybir
+from concourse.masks import make_identity
 
 K, L, R, N, T, J = 512, 1024, 512, 256, 2048, 1024
 FLOPS = 2 * J * (2 * K * R + 2 * L * R + 2 * R * N)
@@ -26,8 +27,8 @@ LAST = CHUNKS - 1
 FIRST_GATHER = 2 * CHUNK
 AHEAD = 2
 LAG = 2
-SECOND_PASS_ROWS = 16
-ENTITY_ROWS = 8
+LANDING = 96
+WEIGHT_ROWS = 8
 ROWS_ON_SYNC = 2
 VECTOR_CAST = P // 2
 
@@ -53,12 +54,14 @@ def tile_list_ckg_sig_kernel(
         tab2_s = kept([P, T], U8, "tab2_s")
         we_s = kept([P, R], U8, "we_s")
         raw = [kept([P, 4, R], F32, f"raw{i}") for i in range(4)]
-        v2_s1 = kept([P, J], U8, "v2_s1")
+        v2_s = [kept([P, J], U8, f"v2_s{a}") for a in range(2)]
+        ident = kept([P, P], F32, "ident")
 
-        nc.gpsimd.memset(tab2_s[:].bitcast(I32), 0)
+        nc.gpsimd.memset(tab2_s[0:LANDING].bitcast(I32), 0)
         nc.gpsimd.memset(we_s[:].bitcast(I32), 0)
         nc.vector.memset(tab_s[:].bitcast(I32), 0)
-        nc.vector.memset(v2_s1[:].bitcast(I32), 0)
+        for a in range(2):
+            nc.vector.memset(v2_s[a][:].bitcast(I32), 0)
 
         def as_words(words):
             return words[0].rearrange("p c i -> p (c i)").bitcast(I32)
@@ -70,35 +73,37 @@ def tile_list_ckg_sig_kernel(
         def load_scale_rows(queue, dst, first, r, rows):
             queue.dma_start(out=dst[first + r : P : QUAD].bitcast(I32), in_=rows[r:16:4].bitcast(I32))
 
-        def load_table2_half(h):
-            cols = slice(h * T // 2, (h + 1) * T // 2)
-            nc.sync.dma_start(out=tab2_w[:, cols].bitcast(I32), in_=as_words(tab2_words)[:, cols])
+        picked2 = kept([P, J], U8, "picked2")
 
-        load_table2_half(0)
+        def move_scale_rows(a):
+            for r in range(4):
+                first = LANDING + 16 * a + r
+                nc.sync.dma_start(
+                    out=v2_s[a][r:P:QUAD].bitcast(I32), in_=picked2[first : first + 13 : 4].bitcast(I32)
+                )
+
         nc.sync.dma_start(list2[:], offs2)
-        for r in range(4):
-            rows = tab2_scales.rearrange("a (q r) t -> r q a t", r=4)[r]
-            nc.sync.dma_start(out=tab2_s[r:P:SECOND_PASS_ROWS, :].bitcast(I32), in_=rows.bitcast(I32))
-        load_table2_half(1)
+        nc.sync.dma_start(
+            out=tab2_s[LANDING:P].bitcast(I32), in_=tab2_scales.rearrange("a q t -> (a q) t").bitcast(I32)
+        )
+        nc.sync.dma_start(out=tab2_w[:].bitcast(I32), in_=as_words(tab2_words))
         load_float_pass(0)
-        load_float_pass(1)
         nc.sync.dma_start(list1[:], offs)
         for r in range(4):
-            load_scale_rows(nc.sync, tab_s, ENTITY_ROWS, r, tab_scales[0])
+            load_scale_rows(nc.sync, tab_s, 0, r, tab_scales[0])
+        load_float_pass(1)
+        nc.vector.tensor_copy(picked2[:], tab2_s[:].indirect(list2[:]))
+        move_scale_rows(0)
         load_float_pass(2)
+        move_scale_rows(1)
         load_float_pass(3)
-        v2_s0 = kept([P, J], U8, "v2_s0")
-        nc.vector.tensor_copy(v2_s0[:], tab2_s[:].indirect(list2[:]))
-        for r in range(4):
-            nc.sync.dma_start(
-                out=v2_s1[r:P:QUAD].bitcast(I32), in_=v2_s0[SECOND_PASS_ROWS + r : P : QUAD].bitcast(I32)
-            )
         for n in range(8):
-            if n == 2:
+            if n == ROWS_ON_SYNC:
                 nc.sync.dma_start(out=tab_w[:].bitcast(I32), in_=as_words(tab_words))
             e, r = divmod(n, 4)
             queue = nc.sync if n < ROWS_ON_SYNC else nc.gpsimd
-            load_scale_rows(queue, we_s, ENTITY_ROWS + 4 * e, r, (wer_scales, wei_scales)[e][0])
+            load_scale_rows(queue, we_s, WEIGHT_ROWS + 4 * e, r, (wer_scales, wei_scales)[e][0])
+        make_identity(nc, ident[:])
 
         v_s = kept([P, J], U8, "v_s")
         v_w = {}
@@ -129,9 +134,9 @@ def tile_list_ckg_sig_kernel(
                 in_=we_w[e][:].bitcast(U32).rearrange("p (g i t) -> p g t i", i=4, t=4),
             )
 
-        def gather_table_words(piece, tag):
+        def gather_table_words(piece):
             j0, j1 = ((0, FIRST_GATHER), (FIRST_GATHER, J))[piece]
-            v_w[piece] = kept([P, j1 - j0], U32, f"v_w{piece}", tag)
+            v_w[piece] = kept([P, j1 - j0], U32, f"v_w{piece}")
             nc.vector.tensor_copy(v_w[piece][:], tab_w[:].indirect(list1[:, j0 // 16 : j1 // 16]))
 
         ae = {}
@@ -145,9 +150,9 @@ def tile_list_ckg_sig_kernel(
                     nc.tensor.matmul_mx(
                         out=bank[:, t, :],
                         lhsT=we_dealt_w[e][:, t, :].bitcast(FP8X4),
-                        lhsT_scale=we_dealt_s[ENTITY_ROWS + 4 * e :, t, :],
+                        lhsT_scale=we_dealt_s[WEIGHT_ROWS + 4 * e :, t, :],
                         rhs=v_w[piece][:, j0 : j0 + CHUNK].bitcast(FP8X4),
-                        rhs_scale=v_s[ENTITY_ROWS:, c * CHUNK : (c + 1) * CHUNK],
+                        rhs_scale=v_s[:, c * CHUNK : (c + 1) * CHUNK],
                         start=True,
                         stop=True,
                     )
@@ -163,7 +168,7 @@ def tile_list_ckg_sig_kernel(
                         lhsT=wr_w[2 * e + a][:, t, :].bitcast(FP8X4),
                         lhsT_scale=wr_s[2 * e + a][:, t, :],
                         rhs=v2_w[:, a, c * CHUNK : (c + 1) * CHUNK].bitcast(FP4X4),
-                        rhs_scale=(v2_s0, v2_s1)[a][:, c * CHUNK : (c + 1) * CHUNK],
+                        rhs_scale=v2_s[a][:, c * CHUNK : (c + 1) * CHUNK],
                         start=(a, t) == (0, 0),
                         stop=(a, t) == (1, 3),
                     )
@@ -172,7 +177,7 @@ def tile_list_ckg_sig_kernel(
         def products(c):
             banks = [relation(c, e) for e in range(2)]
             prods = [ring.tile([P, 2, CHUNK, 4], F32, name=f"prod{e}") for e in range(2)]
-            steps = ((0, 0, 1), (1, 1, 1), (0, 1, 1), (1, 0, 1)) if c == 0 else ((0, 0, 2), (1, 0, 2))
+            steps = ((0, 0, 1), (1, 1, 1), (0, 1, 1), (1, 0, 1)) if c == 1 else ((0, 0, 2), (1, 0, 2))
             for e, o, width in steps:
                 nc.vector.tensor_tensor(
                     out=prods[e][:, o : o + width],
@@ -181,6 +186,45 @@ def tile_list_ckg_sig_kernel(
                     op=MULT,
                 )
             return prods
+
+        def turned_relation(c, e):
+            bank = psum.tile([P, R], F32, name=f"turned_ar{e}", tag=f"ar_bank{e}")
+            for a in range(2):
+                nc.tensor.matmul_mx(
+                    out=bank[:],
+                    lhsT=v2_w[:, a, c * CHUNK : (c + 1) * CHUNK].bitcast(FP4X4),
+                    lhsT_scale=v2_s[a][:, c * CHUNK : (c + 1) * CHUNK],
+                    rhs=wr_w[2 * e + a][:].rearrange("p t m -> p (t m)").bitcast(FP8X4),
+                    rhs_scale=wr_s[2 * e + a][:].rearrange("p t m -> p (t m)"),
+                    start=a == 0,
+                    stop=a == 1,
+                )
+            return bank
+
+        def turned_entity(e):
+            bank = psum.tile([P, R], F32, name="turned_ae", tag="ae_bank", bufs=3)
+            nc.tensor.matmul_mx(
+                out=bank[:],
+                lhsT=v_w[0][:, 0:CHUNK].bitcast(FP8X4),
+                lhsT_scale=v_s[:, 0:CHUNK],
+                rhs=we_w[e][:].bitcast(FP8X4),
+                rhs_scale=we_s[WEIGHT_ROWS + 4 * e :, :],
+                start=True,
+                stop=True,
+            )
+            dealt = kept([P, 4, P], F32, f"turned_ae{e}")
+            nc.scalar.copy(out=dealt[:], in_=bank[:].rearrange("p (m t) -> p t m", t=4))
+            return dealt[:].rearrange("p t m -> p (t m)")
+
+        def add_by_transposes(c, part, first, second):
+            bank = psum.tile([P, 4, CHUNK], F32, name="sum_bank", tag="y_bank", bufs=1)
+            for t in range(4):
+                for n, prod in enumerate((first, second)):
+                    nc.tensor.matmul(
+                        out=bank[:, t, :], lhsT=prod[:, t * P : (t + 1) * P], rhs=ident[:],
+                        is_transpose=True, start=n == 0, stop=n == 1,
+                    )
+            nc.scalar.copy(out=hb[c][:, part], in_=bank[:].rearrange("p t j -> p j t"))
 
         out_v = out.rearrange("(g p) j -> p g j", p=P)
 
@@ -237,14 +281,26 @@ def tile_list_ckg_sig_kernel(
         quantize_weight(3)
         nc.vector.tensor_copy(out=we_dealt_s[:], in_=we_s[:].rearrange("p (m t) -> p t m", t=4))
 
-        gather_table_words(0, None)
-        deal_words(0)
-        deal_words(1)
-        for c in range(AHEAD):
-            entity(c)
-        gather_table_words(1, "we_s")
+        arr_bank = turned_relation(0, 0)
+        arr0 = kept([P, R], F32, "arr0", "raw3")
+        nc.scalar.copy(out=arr0[:], in_=arr_bank[:])
+        ari0 = turned_relation(0, 1)
 
-        n_w = kept([P, 2, 2 * N], U8, "n_w", "raw3")
+        gather_table_words(0)
+        gather_table_words(1)
+        deal_words(0)
+        aer0 = turned_entity(0)
+        deal_words(1)
+        aei0 = turned_entity(1)
+        first = [kept([P, R], F32, f"first{n}") for n in range(4)]
+        nc.gpsimd.tensor_tensor(out=first[0][:], in0=aer0, in1=arr0[:], op=MULT)
+        nc.vector.tensor_tensor(out=first[2][:], in0=aer0, in1=ari0[:], op=MULT)
+        nc.vector.scalar_tensor_tensor(out=first[1][:], in0=aei0, scalar=-1.0, in1=ari0[:], op0=MULT, op1=MULT)
+        nc.gpsimd.tensor_tensor(out=first[3][:], in0=aei0, in1=arr0[:], op=MULT)
+        entity(1)
+        entity(2)
+
+        n_w = kept([P, 2, 2 * N], U8, "n_w", "grouped3")
         n_s = kept([P, 2, N], U8, "n_s", "raw1")
         nc.gpsimd.memset(n_s[:].rearrange("p e n -> p (e n)").bitcast(I32), 0)
         for e, (words, scales) in enumerate(((nr_words, nr_scales), (ni_words, ni_scales))):
@@ -252,9 +308,12 @@ def tile_list_ckg_sig_kernel(
             for r in range(4):
                 load_scale_rows(nc.sync, n_s[:, e, :], 0, r, scales[0])
 
-        hb = {}
-        for c in range(CHUNKS):
+        hb = {0: kept([P, 2, CHUNK, 4], BF16, "hb0")}
+        add_by_transposes(0, 0, first[0], first[1])
+        for c in range(1, CHUNKS):
             with_arr, with_ari = products(c)
+            if c == 1:
+                add_by_transposes(0, 1, first[2], first[3])
             if c >= LAG:
                 score(c - LAG)
             if c == LAST:
@@ -266,6 +325,6 @@ def tile_list_ckg_sig_kernel(
             else:
                 hb[c] = kept([P, 2, CHUNK, 4], BF16, f"hb{c}", "hb_end")
             adder = nc.vector if c == LAST else nc.gpsimd
-            for part in (slice(1, 2), slice(0, 1)) if c == 0 else (slice(0, 1), slice(1, 2)) if c == LAST else (slice(0, 2),):
+            for part in (slice(1, 2), slice(0, 1)) if c == 1 else (slice(0, 1), slice(1, 2)) if c == LAST else (slice(0, 2),):
                 adder.tensor_tensor(out=hb[c][:, part], in0=with_arr[:, part], in1=with_ari[:, part], op=ADD)
         score(LAST)

@@ -188,7 +188,8 @@ def tile_list_ckg_sig_kernel(
             return prods
 
         def turned_relation(c, e):
-            bank = psum.tile([P, R], F32, name=f"turned_ar{e}", tag=f"ar_bank{e}")
+            tag, bufs = (("y_bank", 1), ("ar_bank1", 2))[e]
+            bank = psum.tile([P, R], F32, name=f"turned_ar{e}", tag=tag, bufs=bufs)
             for a in range(2):
                 nc.tensor.matmul_mx(
                     out=bank[:],

@@ -160,7 +160,7 @@ def tile_list_ckg_sig_kernel(
             nc.scalar.activation(out=ae[c][:, 0], in_=bank[:].rearrange("p t j -> p j t"), func=COPY, scale=-1.0)
 
         def relation(c, e):
-            bank = psum.tile([P, 4, CHUNK], F32, name=f"ar_bank{e}", tag=f"ar_bank{e}")
+            bank = psum.tile([P, 4, CHUNK], F32, name=f"ar_bank{e}", tag=f"ar_bank{e}_{c % 2}", bufs=1)
             for a in range(2):
                 for t in range(4):
                     nc.tensor.matmul_mx(
@@ -188,8 +188,8 @@ def tile_list_ckg_sig_kernel(
             return prods
 
         def turned_relation(c, e):
-            tag, bufs = (("y_bank", 1), ("ar_bank1", 2))[e]
-            bank = psum.tile([P, R], F32, name=f"turned_ar{e}", tag=tag, bufs=bufs)
+            tag = f"ar_bank{e}_0" if (c, e) != (0, 0) else "y_bank"
+            bank = psum.tile([P, R], F32, name=f"turned_ar{e}", tag=tag, bufs=1)
             for a in range(2):
                 nc.tensor.matmul_mx(
                     out=bank[:],
@@ -202,28 +202,35 @@ def tile_list_ckg_sig_kernel(
                 )
             return bank
 
-        def turned_entity(e):
-            bank = psum.tile([P, R], F32, name="turned_ae", tag="ae_bank", bufs=3)
+        def turned_entity(c, e, dealt):
+            piece, j0 = (0, c * CHUNK) if c * CHUNK < FIRST_GATHER else (1, c * CHUNK - FIRST_GATHER)
+            if c == 0:
+                words, scales, order = we_w[e][:], we_s[:], "p (m t) -> p t m"
+            else:
+                words = we_dealt_w[e][:].rearrange("p t m -> p (t m)")
+                scales, order = we_dealt_s[:].rearrange("p t m -> p (t m)"), "p (t m) -> p t m"
+            tag, bufs = (f"ar_bank{e}_{c % 2}", 1) if c == LAST else ("ae_bank", 3)
+            bank = psum.tile([P, R], F32, name="turned_ae", tag=tag, bufs=bufs)
             nc.tensor.matmul_mx(
                 out=bank[:],
-                lhsT=v_w[0][:, 0:CHUNK].bitcast(FP8X4),
-                lhsT_scale=v_s[:, 0:CHUNK],
-                rhs=we_w[e][:].bitcast(FP8X4),
-                rhs_scale=we_s[WEIGHT_ROWS + 4 * e :, :],
+                lhsT=v_w[piece][:, j0 : j0 + CHUNK].bitcast(FP8X4),
+                lhsT_scale=v_s[:, c * CHUNK : (c + 1) * CHUNK],
+                rhs=words.bitcast(FP8X4),
+                rhs_scale=scales[WEIGHT_ROWS + 4 * e :],
                 start=True,
                 stop=True,
             )
-            dealt = kept([P, 4, P], F32, f"turned_ae{e}")
-            nc.scalar.copy(out=dealt[:], in_=bank[:].rearrange("p (m t) -> p t m", t=4))
-            return dealt[:].rearrange("p t m -> p (t m)")
+            nc.scalar.copy(out=dealt.rearrange("p (t m) -> p t m", t=4), in_=bank[:].rearrange(order, t=4))
+            return dealt
 
         def add_by_transposes(c, part, first, second):
-            bank = psum.tile([P, 4, CHUNK], F32, name="sum_bank", tag="y_bank", bufs=1)
-            for t in range(4):
-                for n, prod in enumerate((first, second)):
+            tag, bufs = ("y_bank", 1) if c == 0 else ("ae_bank", 3)
+            bank = psum.tile([P, 4, CHUNK], F32, name="sum_bank", tag=tag, bufs=bufs)
+            for n, prod in enumerate((first, second)):
+                for t in range(4):
                     nc.tensor.matmul(
                         out=bank[:, t, :], lhsT=prod[:, t * P : (t + 1) * P], rhs=ident[:],
-                        is_transpose=True, start=n == 0, stop=n == 1,
+                        is_transpose=True, start=(n, t) == (0, 0), stop=(n, t) == (1, 3),
                     )
             nc.scalar.copy(out=hb[c][:, part], in_=bank[:].rearrange("p t j -> p j t"))
 
@@ -239,12 +246,12 @@ def tile_list_ckg_sig_kernel(
                     in_=hb[c][:, part].rearrange("p e j t -> p (e j t)"),
                 )
             if c == LAST:
-                banks = [psum.tile([P, 1, CHUNK], F32, name="y_last", tag="ar_bank0") for g in range(2)]
+                banks = [psum.tile([P, 1, CHUNK], F32, name="y_last", tag=f"ar_bank0_{g}", bufs=1) for g in range(2)]
                 sums = [bank[:, 0, :] for bank in banks]
                 order = [(g, e) for e in range(2) for g in range(2)]
             else:
-                tag, bufs = ("ar_bank1", 2) if c == LAST - 1 else ("y_bank", 1)
-                banks = [psum.tile([P, 2, CHUNK], F32, name="y_bank", tag=tag, bufs=bufs)]
+                tag = "ar_bank1_1" if c == LAST - 1 else "y_bank"
+                banks = [psum.tile([P, 2, CHUNK], F32, name="y_bank", tag=tag, bufs=1)]
                 sums = [banks[0][:, g, :] for g in range(2)]
                 order = [(g, e) for g in range(2) for e in range(2)]
             for g, e in order:
@@ -290,9 +297,9 @@ def tile_list_ckg_sig_kernel(
         gather_table_words(0)
         gather_table_words(1)
         deal_words(0)
-        aer0 = turned_entity(0)
+        aer0 = turned_entity(0, 0, kept([P, R], F32, "aer0")[:])
         deal_words(1)
-        aei0 = turned_entity(1)
+        aei0 = turned_entity(0, 1, kept([P, R], F32, "aei0")[:])
         first = [kept([P, R], F32, f"first{n}") for n in range(4)]
         nc.gpsimd.tensor_tensor(out=first[0][:], in0=aer0, in1=arr0[:], op=MULT)
         nc.vector.tensor_tensor(out=first[2][:], in0=aer0, in1=ari0[:], op=MULT)
@@ -311,21 +318,30 @@ def tile_list_ckg_sig_kernel(
 
         hb = {0: kept([P, 2, CHUNK, 4], BF16, "hb0")}
         add_by_transposes(0, 0, first[0], first[1])
-        for c in range(1, CHUNKS):
+        for c in range(1, LAST):
             with_arr, with_ari = products(c)
             if c == 1:
                 add_by_transposes(0, 1, first[2], first[3])
             if c >= LAG:
                 score(c - LAG)
-            if c == LAST:
-                score(c - 1)
-            if c + AHEAD < CHUNKS:
+            if c + AHEAD < LAST:
                 entity(c + AHEAD)
-            if c < LAST - 1:
-                hb[c] = ring.tile([P, 2, CHUNK, 4], BF16, name="hb", bufs=LAG + 2, align_bytes=64)
-            else:
-                hb[c] = kept([P, 2, CHUNK, 4], BF16, f"hb{c}", "hb_end")
-            adder = nc.vector if c == LAST else nc.gpsimd
-            for part in (slice(1, 2), slice(0, 1)) if c == 1 else (slice(0, 1), slice(1, 2)) if c == LAST else (slice(0, 2),):
-                adder.tensor_tensor(out=hb[c][:, part], in0=with_arr[:, part], in1=with_ari[:, part], op=ADD)
-        score(LAST)
+            if c + AHEAD == LAST:
+                pair = kept([P, 2, R], F32, "ae_last")
+                aer, aei = [turned_entity(LAST, e, pair[:, e]) for e in range(2)]
+            hb[c] = ring.tile([P, 2, CHUNK, 4], BF16, name="hb", bufs=LAG + 2, align_bytes=64)
+            for part in (slice(1, 2), slice(0, 1)) if c == 1 else (slice(0, 2),):
+                nc.gpsimd.tensor_tensor(out=hb[c][:, part], in0=with_arr[:, part], in1=with_ari[:, part], op=ADD)
+
+        arr, ari = [turned_relation(LAST, e) for e in range(2)]
+        with_arr, with_ari = [ring.tile([P, 2, R], F32, name=f"prod{e}") for e in range(2)]
+        hb[LAST] = kept([P, 2, CHUNK, 4], BF16, "hb_last")
+        nc.vector.tensor_tensor(out=with_arr[:, 0], in0=aer, in1=arr[:], op=MULT)
+        nc.vector.scalar_tensor_tensor(out=with_ari[:, 0], in0=aei, scalar=-1.0, in1=ari[:], op0=MULT, op1=MULT)
+        nc.vector.tensor_tensor(out=with_arr[:, 1], in0=aei, in1=arr[:], op=MULT)
+        for cols in (slice(0, R // 2), slice(R // 2, R)):
+            nc.vector.tensor_tensor(out=with_ari[:, 1, cols], in0=aer[:, cols], in1=ari[:, cols], op=MULT)
+        for part in range(2):
+            add_by_transposes(LAST, part, with_arr[:, part], with_ari[:, part])
+        for c in range(LAST - LAG, CHUNKS):
+            score(c)

@@ -28,9 +28,10 @@ FIRST_GATHER = 2 * CHUNK
 AHEAD = 2
 LAG = 2
 LANDING = 96
-WEIGHT_ROWS = 8
+ENTITY_ROWS = 8
 ROWS_ON_SYNC = 2
 VECTOR_CAST = P // 2
+SIGN_ON_VECTOR = (2, 3)
 
 
 def tile_list_ckg_sig_kernel(
@@ -90,7 +91,7 @@ def tile_list_ckg_sig_kernel(
         load_float_pass(0)
         nc.sync.dma_start(list1[:], offs)
         for r in range(4):
-            load_scale_rows(nc.sync, tab_s, 0, r, tab_scales[0])
+            load_scale_rows(nc.sync, tab_s, ENTITY_ROWS, r, tab_scales[0])
         load_float_pass(1)
         nc.vector.tensor_copy(picked2[:], tab2_s[:].indirect(list2[:]))
         move_scale_rows(0)
@@ -102,7 +103,7 @@ def tile_list_ckg_sig_kernel(
                 nc.sync.dma_start(out=tab_w[:].bitcast(I32), in_=as_words(tab_words))
             e, r = divmod(n, 4)
             queue = nc.sync if n < ROWS_ON_SYNC else nc.gpsimd
-            load_scale_rows(queue, we_s, WEIGHT_ROWS + 4 * e, r, (wer_scales, wei_scales)[e][0])
+            load_scale_rows(queue, we_s, ENTITY_ROWS * e, r, (wer_scales, wei_scales)[e][0])
         make_identity(nc, ident[:])
 
         v_s = kept([P, J], U8, "v_s")
@@ -150,14 +151,15 @@ def tile_list_ckg_sig_kernel(
                     nc.tensor.matmul_mx(
                         out=bank[:, t, :],
                         lhsT=we_dealt_w[e][:, t, :].bitcast(FP8X4),
-                        lhsT_scale=we_dealt_s[WEIGHT_ROWS + 4 * e :, t, :],
+                        lhsT_scale=we_dealt_s[ENTITY_ROWS * e :, t, :],
                         rhs=v_w[piece][:, j0 : j0 + CHUNK].bitcast(FP8X4),
-                        rhs_scale=v_s[:, c * CHUNK : (c + 1) * CHUNK],
+                        rhs_scale=v_s[ENTITY_ROWS:, c * CHUNK : (c + 1) * CHUNK],
                         start=True,
                         stop=True,
                     )
                 nc.scalar.copy(out=ae[c][:, 1 + e], in_=bank[:].rearrange("p t j -> p j t"))
-            nc.scalar.activation(out=ae[c][:, 0], in_=bank[:].rearrange("p t j -> p j t"), func=COPY, scale=-1.0)
+            if c not in SIGN_ON_VECTOR:
+                nc.scalar.activation(out=ae[c][:, 0], in_=bank[:].rearrange("p t j -> p j t"), func=COPY, scale=-1.0)
 
         def relation(c, e):
             bank = psum.tile([P, 4, CHUNK], F32, name=f"ar_bank{e}", tag=f"ar_bank{e}_{c % 2}", bufs=1)
@@ -177,8 +179,18 @@ def tile_list_ckg_sig_kernel(
         def products(c):
             banks = [relation(c, e) for e in range(2)]
             prods = [ring.tile([P, 2, CHUNK, 4], F32, name=f"prod{e}") for e in range(2)]
-            steps = ((0, 0, 1), (1, 1, 1), (0, 1, 1), (1, 0, 1)) if c == 1 else ((0, 0, 2), (1, 0, 2))
+            if c == 1:
+                steps = ((0, 0, 1), (1, 1, 1), (0, 1, 1), (1, 0, 1))
+            elif c in SIGN_ON_VECTOR:
+                steps = ((0, 0, 2), (1, 1, 1), (1, 0, 1))
+            else:
+                steps = ((0, 0, 2), (1, 0, 2))
             for e, o, width in steps:
+                if (e, o) == (1, 0) and c in SIGN_ON_VECTOR:
+                    nc.vector.scalar_tensor_tensor(
+                        out=prods[1][:, 0], in0=ae[c][:, 2], scalar=-1.0, in1=banks[1][:, 0], op0=MULT, op1=MULT
+                    )
+                    continue
                 nc.vector.tensor_tensor(
                     out=prods[e][:, o : o + width],
                     in0=ae[c][:, 1 - e + o : 1 - e + o + width],
@@ -214,9 +226,9 @@ def tile_list_ckg_sig_kernel(
             nc.tensor.matmul_mx(
                 out=bank[:],
                 lhsT=v_w[piece][:, j0 : j0 + CHUNK].bitcast(FP8X4),
-                lhsT_scale=v_s[:, c * CHUNK : (c + 1) * CHUNK],
+                lhsT_scale=v_s[ENTITY_ROWS:, c * CHUNK : (c + 1) * CHUNK],
                 rhs=words.bitcast(FP8X4),
-                rhs_scale=scales[WEIGHT_ROWS + 4 * e :],
+                rhs_scale=scales[ENTITY_ROWS * e :],
                 start=True,
                 stop=True,
             )
@@ -237,13 +249,15 @@ def tile_list_ckg_sig_kernel(
         out_v = out.rearrange("(g p) j -> p g j", p=P)
 
         def score(c):
-            h_w = ring.tile([P, 2, CHUNK], U32, name="h_w", align_bytes=64)
-            h_s = ring.tile([P, 2, CHUNK], U8, name="h_s", align_bytes=64)
+            width = 2 * CHUNK if c == 0 else CHUNK
+            h_w = ring.tile([P, 2, width], U32, name="h_w", align_bytes=64)
+            h_s = ring.tile([P, 2, width], U8, name="h_s", align_bytes=64)
+            sums_in = first_two if c == 0 else hb[c]
             for part in (slice(0, 1), slice(1, 2)) if c == LAST else (slice(0, 2),):
                 nc.vector.quantize_mx(
                     out=h_w[:, part].rearrange("p e j -> p (e j)").bitcast(FP8X4),
                     scales=h_s[:, part].rearrange("p e j -> p (e j)"),
-                    in_=hb[c][:, part].rearrange("p e j t -> p (e j t)"),
+                    in_=sums_in[:, part].rearrange("p e j t -> p (e j t)"),
                 )
             if c == LAST:
                 banks = [psum.tile([P, 1, CHUNK], F32, name="y_last", tag=f"ar_bank0_{g}", bufs=1) for g in range(2)]
@@ -251,7 +265,7 @@ def tile_list_ckg_sig_kernel(
                 order = [(g, e) for e in range(2) for g in range(2)]
             else:
                 tag = "ar_bank1_1" if c == LAST - 1 else "y_bank"
-                banks = [psum.tile([P, 2, CHUNK], F32, name="y_bank", tag=tag, bufs=1)]
+                banks = [psum.tile([P, 2, width], F32, name="y_bank", tag=tag, bufs=1)]
                 sums = [banks[0][:, g, :] for g in range(2)]
                 order = [(g, e) for g in range(2) for e in range(2)]
             for g, e in order:
@@ -266,10 +280,10 @@ def tile_list_ckg_sig_kernel(
                 )
             groups = 2 // len(banks)
             for g0, bank in enumerate(banks):
-                res = ring.tile([P, groups, CHUNK], F32, name="res", tag="res", bufs=4)
+                res = ring.tile([P, groups, width], F32, name="res", tag="res", bufs=4)
                 nc.scalar.activation(out=res[:], in_=bank[:], func=SIGMOID)
                 queue = nc.scalar if (c, g0) == (LAST, 1) else nc.sync
-                queue.dma_start(out=out_v[:, g0 : g0 + groups, c * CHUNK : (c + 1) * CHUNK], in_=res[:])
+                queue.dma_start(out=out_v[:, g0 : g0 + groups, c * CHUNK : c * CHUNK + width], in_=res[:])
 
         nc.vector.tensor_copy(v2_both[:], tab2_w[:].indirect(list2[:]))
         nc.vector.tensor_copy(v_s[:], tab_s[:].indirect(list1[:]))
@@ -316,20 +330,21 @@ def tile_list_ckg_sig_kernel(
             for r in range(4):
                 load_scale_rows(nc.sync, n_s[:, e, :], 0, r, scales[0])
 
-        hb = {0: kept([P, 2, CHUNK, 4], BF16, "hb0")}
-        add_by_transposes(0, 0, first[0], first[1])
+        first_two = kept([P, 2, 2 * CHUNK, 4], BF16, "first_two")
+        hb = {c: first_two[:, :, c * CHUNK : (c + 1) * CHUNK] for c in range(2)}
         for c in range(1, LAST):
             with_arr, with_ari = products(c)
-            if c == 1:
-                add_by_transposes(0, 1, first[2], first[3])
-            if c >= LAG:
-                score(c - LAG)
+            if c > LAG:
+                score(0 if c == LAG + 1 else c - LAG)
             if c + AHEAD < LAST:
                 entity(c + AHEAD)
+            if c <= 2:
+                add_by_transposes(0, c - 1, first[2 * c - 2], first[2 * c - 1])
             if c + AHEAD == LAST:
                 pair = kept([P, 2, R], F32, "ae_last")
                 aer, aei = [turned_entity(LAST, e, pair[:, e]) for e in range(2)]
-            hb[c] = ring.tile([P, 2, CHUNK, 4], BF16, name="hb", bufs=LAG + 2, align_bytes=64)
+            if c > 1:
+                hb[c] = ring.tile([P, 2, CHUNK, 4], BF16, name="hb", bufs=LAG + 2, align_bytes=64)
             for part in (slice(1, 2), slice(0, 1)) if c == 1 else (slice(0, 2),):
                 nc.gpsimd.tensor_tensor(out=hb[c][:, part], in0=with_arr[:, part], in1=with_ari[:, part], op=ADD)
 

@@ -31,7 +31,7 @@ LANDING = 96
 ENTITY_ROWS = 8
 ROWS_ON_SYNC = 2
 VECTOR_CAST = P // 2
-SIGN_ON_VECTOR = (2, 3)
+SIGN_ON_VECTOR = range(2, LAST)
 
 
 def tile_list_ckg_sig_kernel(
@@ -60,6 +60,9 @@ def tile_list_ckg_sig_kernel(
 
         nc.gpsimd.memset(tab2_s[0:LANDING].bitcast(I32), 0)
         nc.gpsimd.memset(we_s[:].bitcast(I32), 0)
+        warm = kept([P, 2], F32, "warm")
+        nc.gpsimd.memset(warm[:, 0:1], 0.0)
+        nc.scalar.activation(out=warm[:, 1:2], in_=warm[:, 0:1], func=SIGMOID)
         nc.vector.memset(tab_s[:].bitcast(I32), 0)
         for a in range(2):
             nc.vector.memset(v2_s[a][:].bitcast(I32), 0)
@@ -113,7 +116,7 @@ def tile_list_ckg_sig_kernel(
         we_dealt_w = [kept([P, 4, P], U32, f"we_dealt_w{e}") for e in range(2)]
         we_dealt_s = kept([P, 4, P], U8, "we_dealt_s")
         grouped = [kept([P, 4, P, 4], BF16, f"grouped{i}") for i in range(4)]
-        wr_w = [kept([P, 4, P], U32, f"wr_w{i}") for i in range(4)]
+        wr_w = {}
         wr_s = [kept([P, 4, P], U8, f"wr_s{i}") for i in range(4)]
 
         def cast(copy, i, m0, m1):
@@ -123,6 +126,7 @@ def tile_list_ckg_sig_kernel(
             )
 
         def quantize_weight(i):
+            wr_w[i] = kept([P, 4, P], U32, f"wr_w{i}", "tab_s" if i == 0 else None)
             nc.vector.quantize_mx(
                 out=wr_w[i][:].rearrange("p t m -> p (t m)").bitcast(FP8X4),
                 scales=wr_s[i][:].rearrange("p t m -> p (t m)"),

@@ -27,7 +27,7 @@ LAST = CHUNKS - 1
 FIRST_GATHER = 2 * CHUNK
 AHEAD = 2
 LAG = 2
-LANDING = 96
+LANDING = (112, 48)
 ENTITY_ROWS = 8
 ROWS_ON_SYNC = 2
 VECTOR_CAST = P // 2
@@ -58,7 +58,8 @@ def tile_list_ckg_sig_kernel(
         v2_s = [kept([P, J], U8, f"v2_s{a}") for a in range(2)]
         ident = kept([P, P], F32, "ident")
 
-        nc.gpsimd.memset(tab2_s[0:LANDING].bitcast(I32), 0)
+        nc.gpsimd.memset(tab2_s[0 : LANDING[1]].bitcast(I32), 0)
+        nc.gpsimd.memset(tab2_s[P // 2 : LANDING[0]].bitcast(I32), 0)
         nc.gpsimd.memset(we_s[:].bitcast(I32), 0)
         warm = kept([P, 2], F32, "warm")
         nc.gpsimd.memset(warm[:, 0:1], 0.0)
@@ -81,15 +82,14 @@ def tile_list_ckg_sig_kernel(
 
         def move_scale_rows(a):
             for r in range(4):
-                first = LANDING + 16 * a + r
+                first = LANDING[a] + r
                 nc.sync.dma_start(
                     out=v2_s[a][r:P:QUAD].bitcast(I32), in_=picked2[first : first + 13 : 4].bitcast(I32)
                 )
 
         nc.sync.dma_start(list2[:], offs2)
-        nc.sync.dma_start(
-            out=tab2_s[LANDING:P].bitcast(I32), in_=tab2_scales.rearrange("a q t -> (a q) t").bitcast(I32)
-        )
+        for a in range(2):
+            nc.sync.dma_start(out=tab2_s[LANDING[a] : LANDING[a] + 16].bitcast(I32), in_=tab2_scales[a].bitcast(I32))
         nc.sync.dma_start(out=tab2_w[:].bitcast(I32), in_=as_words(tab2_words))
         load_float_pass(0)
         nc.sync.dma_start(list1[:], offs)

@@ -27,11 +27,10 @@ LAST = CHUNKS - 1
 FIRST_GATHER = 2 * CHUNK
 AHEAD = 2
 LAG = 2
-LANDING = (112, 48)
+LANDING = 96
 ENTITY_ROWS = 8
-ROWS_ON_SYNC = 2
 VECTOR_CAST = P // 2
-SIGN_ON_VECTOR = range(2, LAST)
+SIGN_ON_VECTOR = range(1, LAST)
 
 
 def tile_list_ckg_sig_kernel(
@@ -58,8 +57,7 @@ def tile_list_ckg_sig_kernel(
         v2_s = [kept([P, J], U8, f"v2_s{a}") for a in range(2)]
         ident = kept([P, P], F32, "ident")
 
-        nc.gpsimd.memset(tab2_s[0 : LANDING[1]].bitcast(I32), 0)
-        nc.gpsimd.memset(tab2_s[P // 2 : LANDING[0]].bitcast(I32), 0)
+        nc.gpsimd.memset(tab2_s[0:LANDING].bitcast(I32), 0)
         nc.gpsimd.memset(we_s[:].bitcast(I32), 0)
         warm = kept([P, 2], F32, "warm")
         nc.gpsimd.memset(warm[:, 0:1], 0.0)
@@ -75,38 +73,37 @@ def tile_list_ckg_sig_kernel(
             rows = (wrr, wri)[i // 2][512 * (i % 2) : 512 * (i % 2 + 1), :]
             nc.sync.dma_start(out=raw[i][:], in_=rows.rearrange("(p j) c -> p j c", j=4))
 
-        def load_scale_rows(queue, dst, first, r, rows):
-            queue.dma_start(out=dst[first + r : P : QUAD].bitcast(I32), in_=rows[r:16:4].bitcast(I32))
+        def load_scale_rows(dst, first, r, rows):
+            nc.sync.dma_start(out=dst[first + r : P : QUAD].bitcast(I32), in_=rows[r:16:4].bitcast(I32))
 
         picked2 = kept([P, J], U8, "picked2")
 
         def move_scale_rows(a):
             for r in range(4):
-                first = LANDING[a] + r
+                first = LANDING + 16 * a + r
                 nc.sync.dma_start(
                     out=v2_s[a][r:P:QUAD].bitcast(I32), in_=picked2[first : first + 13 : 4].bitcast(I32)
                 )
 
         nc.sync.dma_start(list2[:], offs2)
-        for a in range(2):
-            nc.sync.dma_start(out=tab2_s[LANDING[a] : LANDING[a] + 16].bitcast(I32), in_=tab2_scales[a].bitcast(I32))
+        nc.sync.dma_start(
+            out=tab2_s[LANDING:P].bitcast(I32), in_=tab2_scales.rearrange("a q t -> (a q) t").bitcast(I32)
+        )
         nc.sync.dma_start(out=tab2_w[:].bitcast(I32), in_=as_words(tab2_words))
         load_float_pass(0)
         nc.sync.dma_start(list1[:], offs)
         for r in range(4):
-            load_scale_rows(nc.sync, tab_s, ENTITY_ROWS, r, tab_scales[0])
+            load_scale_rows(tab_s, ENTITY_ROWS, r, tab_scales[0])
         load_float_pass(1)
         nc.vector.tensor_copy(picked2[:], tab2_s[:].indirect(list2[:]))
-        move_scale_rows(0)
-        load_float_pass(2)
-        move_scale_rows(1)
-        load_float_pass(3)
-        for n in range(8):
-            if n == ROWS_ON_SYNC:
-                nc.sync.dma_start(out=tab_w[:].bitcast(I32), in_=as_words(tab_words))
-            e, r = divmod(n, 4)
-            queue = nc.sync if n < ROWS_ON_SYNC else nc.gpsimd
-            load_scale_rows(queue, we_s, ENTITY_ROWS * e, r, (wer_scales, wei_scales)[e][0])
+        for a in range(2):
+            move_scale_rows(a)
+            for r in (2 * a, 2 * a + 1):
+                load_scale_rows(we_s, 0, r, wer_scales[0])
+            load_float_pass(2 + a)
+        for r in range(4):
+            load_scale_rows(we_s, ENTITY_ROWS, r, wei_scales[0])
+        nc.sync.dma_start(out=tab_w[:].bitcast(I32), in_=as_words(tab_words))
         make_identity(nc, ident[:])
 
         v_s = kept([P, J], U8, "v_s")
@@ -240,8 +237,7 @@ def tile_list_ckg_sig_kernel(
             return dealt
 
         def add_by_transposes(c, part, first, second):
-            tag, bufs = ("y_bank", 1) if c == 0 else ("ae_bank", 3)
-            bank = psum.tile([P, 4, CHUNK], F32, name="sum_bank", tag=tag, bufs=bufs)
+            bank = psum.tile([P, 4, CHUNK], F32, name="sum_bank", tag="ae_bank", bufs=3)
             for n, prod in enumerate((first, second)):
                 for t in range(4):
                     nc.tensor.matmul(
@@ -332,7 +328,7 @@ def tile_list_ckg_sig_kernel(
         for e, (words, scales) in enumerate(((nr_words, nr_scales), (ni_words, ni_scales))):
             nc.sync.dma_start(out=n_w[:, e, :].bitcast(I32), in_=words[0].bitcast(I32))
             for r in range(4):
-                load_scale_rows(nc.sync, n_s[:, e, :], 0, r, scales[0])
+                load_scale_rows(n_s[:, e, :], 0, r, scales[0])
 
         first_two = kept([P, 2, 2 * CHUNK, 4], BF16, "first_two")
         hb = {c: first_two[:, :, c * CHUNK : (c + 1) * CHUNK] for c in range(2)}

@@ -16,7 +16,6 @@ FP8X4 = mybir.dt.float8_e4m3fn_x4
 FP4X4 = mybir.dt.float4_e2m1fn_x4
 MULT = mybir.AluOpType.mult
 ADD = mybir.AluOpType.add
-COPY = mybir.ActivationFunctionType.Copy
 SIGMOID = mybir.ActivationFunctionType.Sigmoid
 
 P = 128
@@ -29,8 +28,7 @@ AHEAD = 2
 LAG = 2
 LANDING = 96
 ENTITY_ROWS = 8
-VECTOR_CAST = P // 2
-SIGN_ON_VECTOR = range(1, LAST)
+VECTOR_CAST = {2: 3 * P // 8, 3: 5 * P // 8}
 
 
 def tile_list_ckg_sig_kernel(
@@ -41,10 +39,25 @@ def tile_list_ckg_sig_kernel(
     with ExitStack() as ctx:
         keep = ctx.enter_context(tc.tile_pool(name="keep", bufs=1))
         ring = ctx.enter_context(tc.tile_pool(name="ring", bufs=3))
-        psum = ctx.enter_context(tc.psum_pool(name="psum", bufs=2))
+        psum = ctx.enter_context(tc.psum_pool(name="psum", bufs=1))
 
         def kept(shape, dtype, name, tag=None):
             return keep.tile(shape, dtype, name=name, tag=tag or name, align_bytes=64)
+
+        def entity_bank(name):
+            return psum.tile([P, R], F32, name=name, tag="entity_bank", bufs=3)
+
+        def relation_bank(name, e, turn):
+            return psum.tile([P, R], F32, name=name, tag=f"relation_bank{e}_{turn}")
+
+        def score_bank(name):
+            return psum.tile([P, R], F32, name=name, tag="score_bank")
+
+        def cols(c):
+            return slice(c * CHUNK, (c + 1) * CHUNK)
+
+        def by_entry(ap):
+            return ap.rearrange("p (t j) -> p j t", t=4)
 
         list1 = keep.tile([P, J // 16], U16, name="list1")
         list2 = keep.tile([P, J // 16], U16, name="list2")
@@ -110,11 +123,11 @@ def tile_list_ckg_sig_kernel(
         v_w = {}
         v2_both = kept([P, J], U32, "v2_both")
         v2_w = kept([P, 2, J], U16, "v2_w")
-        we_dealt_w = [kept([P, 4, P], U32, f"we_dealt_w{e}") for e in range(2)]
-        we_dealt_s = kept([P, 4, P], U8, "we_dealt_s")
+        we_dealt_w = [kept([P, R], U32, f"we_dealt_w{e}") for e in range(2)]
+        we_dealt_s = kept([P, R], U8, "we_dealt_s")
         grouped = [kept([P, 4, P, 4], BF16, f"grouped{i}") for i in range(4)]
         wr_w = {}
-        wr_s = [kept([P, 4, P], U8, f"wr_s{i}") for i in range(4)]
+        wr_s = [kept([P, R], U8, f"wr_s{i}") for i in range(4)]
 
         def cast(copy, i, m0, m1):
             copy(
@@ -122,17 +135,19 @@ def tile_list_ckg_sig_kernel(
                 in_=raw[i][:].rearrange("p j (m t) -> p m j t", t=4)[:, m0:m1, :, :],
             )
 
+        def shared_cast(i):
+            cast(nc.vector.tensor_copy, i, 0, VECTOR_CAST[i])
+            cast(nc.scalar.copy, i, VECTOR_CAST[i], P)
+
         def quantize_weight(i):
-            wr_w[i] = kept([P, 4, P], U32, f"wr_w{i}", "tab_s" if i == 0 else None)
+            wr_w[i] = kept([P, R], U32, f"wr_w{i}", "tab_s" if i == 0 else None)
             nc.vector.quantize_mx(
-                out=wr_w[i][:].rearrange("p t m -> p (t m)").bitcast(FP8X4),
-                scales=wr_s[i][:].rearrange("p t m -> p (t m)"),
-                in_=grouped[i][:].rearrange("p t m j -> p (t m j)"),
+                out=wr_w[i][:].bitcast(FP8X4), scales=wr_s[i][:], in_=grouped[i][:].rearrange("p t m j -> p (t m j)")
             )
 
         def deal_words(e):
             nc.scalar.copy(
-                out=we_dealt_w[e][:].rearrange("p t (g i) -> p g t i", i=4),
+                out=we_dealt_w[e][:].rearrange("p (t g i) -> p g t i", t=4, i=4),
                 in_=we_w[e][:].bitcast(U32).rearrange("p (g i t) -> p g t i", i=4, t=4),
             )
 
@@ -141,147 +156,115 @@ def tile_list_ckg_sig_kernel(
             v_w[piece] = kept([P, j1 - j0], U32, f"v_w{piece}")
             nc.vector.tensor_copy(v_w[piece][:], tab_w[:].indirect(list1[:, j0 // 16 : j1 // 16]))
 
+        def entity_columns(c):
+            piece, j0 = (0, c * CHUNK) if c * CHUNK < FIRST_GATHER else (1, c * CHUNK - FIRST_GATHER)
+            return v_w[piece][:, j0 : j0 + CHUNK].bitcast(FP8X4), v_s[ENTITY_ROWS:, cols(c)]
+
         ae = {}
 
         def entity(c):
-            piece, j0 = (0, c * CHUNK) if c * CHUNK < FIRST_GATHER else (1, c * CHUNK - FIRST_GATHER)
-            ae[c] = ring.tile([P, 3, CHUNK, 4], F32, name="ae", bufs=AHEAD)
+            words, scales = entity_columns(c)
+            pair = ring.tile([P, 2, CHUNK, 4], F32, name="ae", bufs=AHEAD)
+            ae[c] = [pair[:, 0], pair[:, 1], pair[:]]
             for e in range(2):
-                bank = psum.tile([P, 4, CHUNK], F32, name="ae_bank", bufs=3)
+                bank = entity_bank("ae_bank")
                 for t in range(4):
                     nc.tensor.matmul_mx(
-                        out=bank[:, t, :],
-                        lhsT=we_dealt_w[e][:, t, :].bitcast(FP8X4),
-                        lhsT_scale=we_dealt_s[ENTITY_ROWS * e :, t, :],
-                        rhs=v_w[piece][:, j0 : j0 + CHUNK].bitcast(FP8X4),
-                        rhs_scale=v_s[ENTITY_ROWS:, c * CHUNK : (c + 1) * CHUNK],
-                        start=True,
-                        stop=True,
+                        out=bank[:, cols(t)], lhsT=we_dealt_w[e][:, cols(t)].bitcast(FP8X4),
+                        lhsT_scale=we_dealt_s[ENTITY_ROWS * e :, cols(t)], rhs=words, rhs_scale=scales,
+                        start=True, stop=True,
                     )
-                nc.scalar.copy(out=ae[c][:, 1 + e], in_=bank[:].rearrange("p t j -> p j t"))
-            if c not in SIGN_ON_VECTOR:
-                nc.scalar.activation(out=ae[c][:, 0], in_=bank[:].rearrange("p t j -> p j t"), func=COPY, scale=-1.0)
+                nc.scalar.copy(out=ae[c][e], in_=by_entry(bank[:]))
 
         def relation(c, e):
-            bank = psum.tile([P, 4, CHUNK], F32, name=f"ar_bank{e}", tag=f"ar_bank{e}_{c % 2}", bufs=1)
+            bank = relation_bank("ar_bank", e, c % 2)
             for a in range(2):
                 for t in range(4):
                     nc.tensor.matmul_mx(
-                        out=bank[:, t, :],
-                        lhsT=wr_w[2 * e + a][:, t, :].bitcast(FP8X4),
-                        lhsT_scale=wr_s[2 * e + a][:, t, :],
-                        rhs=v2_w[:, a, c * CHUNK : (c + 1) * CHUNK].bitcast(FP4X4),
-                        rhs_scale=v2_s[a][:, c * CHUNK : (c + 1) * CHUNK],
-                        start=(a, t) == (0, 0),
-                        stop=(a, t) == (1, 3),
+                        out=bank[:, cols(t)], lhsT=wr_w[2 * e + a][:, cols(t)].bitcast(FP8X4),
+                        lhsT_scale=wr_s[2 * e + a][:, cols(t)], rhs=v2_w[:, a, cols(c)].bitcast(FP4X4),
+                        rhs_scale=v2_s[a][:, cols(c)], start=(a, t) == (0, 0), stop=(a, t) == (1, 3),
                     )
-            return bank[:].rearrange("p t j -> p j t").unsqueeze(1)
+            return by_entry(bank[:])
+
+        def times(out, first, second):
+            nc.vector.tensor_tensor(out=out, in0=first, in1=second, op=MULT)
+
+        def minus_times(out, first, second):
+            nc.vector.scalar_tensor_tensor(out=out, in0=first, scalar=-1.0, in1=second, op0=MULT, op1=MULT)
 
         def products(c):
-            banks = [relation(c, e) for e in range(2)]
-            prods = [ring.tile([P, 2, CHUNK, 4], F32, name=f"prod{e}") for e in range(2)]
+            aer, aei, pair = ae[c]
+            arr, ari = [relation(c, e) for e in range(2)]
+            with_arr, with_ari = [ring.tile([P, 2, CHUNK, 4], F32, name=f"prod{e}") for e in range(2)]
             if c == 1:
-                steps = ((0, 0, 1), (1, 1, 1), (0, 1, 1), (1, 0, 1))
-            elif c in SIGN_ON_VECTOR:
-                steps = ((0, 0, 2), (1, 1, 1), (1, 0, 1))
+                times(with_arr[:, 0], aer, arr)
+                times(with_ari[:, 1], aer, ari)
+                times(with_arr[:, 1], aei, arr)
             else:
-                steps = ((0, 0, 2), (1, 0, 2))
-            for e, o, width in steps:
-                if (e, o) == (1, 0) and c in SIGN_ON_VECTOR:
-                    nc.vector.scalar_tensor_tensor(
-                        out=prods[1][:, 0], in0=ae[c][:, 2], scalar=-1.0, in1=banks[1][:, 0], op0=MULT, op1=MULT
-                    )
-                    continue
-                nc.vector.tensor_tensor(
-                    out=prods[e][:, o : o + width],
-                    in0=ae[c][:, 1 - e + o : 1 - e + o + width],
-                    in1=banks[e].to_broadcast([P, width, CHUNK, 4]),
-                    op=MULT,
-                )
-            return prods
+                times(with_arr[:], pair, arr.unsqueeze(1).to_broadcast([P, 2, CHUNK, 4]))
+                times(with_ari[:, 1], aer, ari)
+            minus_times(with_ari[:, 0], aei, ari)
+            return with_arr, with_ari
 
-        def turned_relation(c, e):
-            tag = f"ar_bank{e}_0" if (c, e) != (0, 0) else "y_bank"
-            bank = psum.tile([P, R], F32, name=f"turned_ar{e}", tag=tag, bufs=1)
+        def turned_relation(c, e, bank):
             for a in range(2):
                 nc.tensor.matmul_mx(
-                    out=bank[:],
-                    lhsT=v2_w[:, a, c * CHUNK : (c + 1) * CHUNK].bitcast(FP4X4),
-                    lhsT_scale=v2_s[a][:, c * CHUNK : (c + 1) * CHUNK],
-                    rhs=wr_w[2 * e + a][:].rearrange("p t m -> p (t m)").bitcast(FP8X4),
-                    rhs_scale=wr_s[2 * e + a][:].rearrange("p t m -> p (t m)"),
-                    start=a == 0,
-                    stop=a == 1,
+                    out=bank[:], lhsT=v2_w[:, a, cols(c)].bitcast(FP4X4), lhsT_scale=v2_s[a][:, cols(c)],
+                    rhs=wr_w[2 * e + a][:].bitcast(FP8X4), rhs_scale=wr_s[2 * e + a][:], start=a == 0, stop=a == 1,
                 )
-            return bank
+            return bank[:]
 
-        def turned_entity(c, e, dealt):
-            piece, j0 = (0, c * CHUNK) if c * CHUNK < FIRST_GATHER else (1, c * CHUNK - FIRST_GATHER)
-            if c == 0:
-                words, scales, order = we_w[e][:], we_s[:], "p (m t) -> p t m"
-            else:
-                words = we_dealt_w[e][:].rearrange("p t m -> p (t m)")
-                scales, order = we_dealt_s[:].rearrange("p t m -> p (t m)"), "p (t m) -> p t m"
-            tag, bufs = (f"ar_bank{e}_{c % 2}", 1) if c == LAST else ("ae_bank", 3)
-            bank = psum.tile([P, R], F32, name="turned_ae", tag=tag, bufs=bufs)
+        def turned_entity(c, e, bank, weight_words, weight_scales):
+            words, scales = entity_columns(c)
             nc.tensor.matmul_mx(
-                out=bank[:],
-                lhsT=v_w[piece][:, j0 : j0 + CHUNK].bitcast(FP8X4),
-                lhsT_scale=v_s[ENTITY_ROWS:, c * CHUNK : (c + 1) * CHUNK],
-                rhs=words.bitcast(FP8X4),
-                rhs_scale=scales[ENTITY_ROWS * e :],
-                start=True,
-                stop=True,
+                out=bank[:], lhsT=words, lhsT_scale=scales, rhs=weight_words[:].bitcast(FP8X4),
+                rhs_scale=weight_scales[ENTITY_ROWS * e :], start=True, stop=True,
             )
-            nc.scalar.copy(out=dealt.rearrange("p (t m) -> p t m", t=4), in_=bank[:].rearrange(order, t=4))
-            return dealt
+            return bank[:]
 
         def add_by_transposes(c, part, first, second):
-            bank = psum.tile([P, 4, CHUNK], F32, name="sum_bank", tag="ae_bank", bufs=3)
+            bank = entity_bank("sum_bank")
             for n, prod in enumerate((first, second)):
                 for t in range(4):
                     nc.tensor.matmul(
-                        out=bank[:, t, :], lhsT=prod[:, t * P : (t + 1) * P], rhs=ident[:],
+                        out=bank[:, cols(t)], lhsT=prod[:, cols(t)], rhs=ident[:],
                         is_transpose=True, start=(n, t) == (0, 0), stop=(n, t) == (1, 3),
                     )
-            nc.scalar.copy(out=hb[c][:, part], in_=bank[:].rearrange("p t j -> p j t"))
+            nc.scalar.copy(out=hb[c][:, part], in_=by_entry(bank[:]))
 
         out_v = out.rearrange("(g p) j -> p g j", p=P)
 
         def score(c):
             width = 2 * CHUNK if c == 0 else CHUNK
+            rounded = first_two if c == 0 else hb[c]
             h_w = ring.tile([P, 2, width], U32, name="h_w", align_bytes=64)
             h_s = ring.tile([P, 2, width], U8, name="h_s", align_bytes=64)
-            sums_in = first_two if c == 0 else hb[c]
             for part in (slice(0, 1), slice(1, 2)) if c == LAST else (slice(0, 2),):
                 nc.vector.quantize_mx(
                     out=h_w[:, part].rearrange("p e j -> p (e j)").bitcast(FP8X4),
                     scales=h_s[:, part].rearrange("p e j -> p (e j)"),
-                    in_=sums_in[:, part].rearrange("p e j t -> p (e j t)"),
+                    in_=rounded[:, part].rearrange("p e j t -> p (e j t)"),
                 )
             if c == LAST:
-                banks = [psum.tile([P, 1, CHUNK], F32, name="y_last", tag=f"ar_bank0_{g}", bufs=1) for g in range(2)]
-                sums = [bank[:, 0, :] for bank in banks]
+                banks = [relation_bank("y_last", 0, g)[:, 0:width] for g in range(2)]
+                sums = banks
                 order = [(g, e) for e in range(2) for g in range(2)]
             else:
-                tag = "ar_bank1_1" if c == LAST - 1 else "y_bank"
-                banks = [psum.tile([P, 2, width], F32, name="y_bank", tag=tag, bufs=1)]
-                sums = [banks[0][:, g, :] for g in range(2)]
+                bank = relation_bank("y_bank", 1, 1) if c == LAST - 1 else score_bank("y_bank")
+                banks = [bank[:, 0 : 2 * width]]
+                sums = [bank[:, g * width : (g + 1) * width] for g in range(2)]
                 order = [(g, e) for g in range(2) for e in range(2)]
             for g, e in order:
                 nc.tensor.matmul_mx(
-                    out=sums[g],
-                    lhsT=n_w[:, e, 2 * P * g : 2 * P * (g + 1)].bitcast(FP4X4),
-                    lhsT_scale=n_s[:, e, P * g : P * (g + 1)],
-                    rhs=h_w[:, e, :].bitcast(FP8X4),
-                    rhs_scale=h_s[:, e, :],
-                    start=(e == 0),
-                    stop=(e == 1),
+                    out=sums[g], lhsT=n_w[:, e, 2 * P * g : 2 * P * (g + 1)].bitcast(FP4X4),
+                    lhsT_scale=n_s[:, e, cols(g)], rhs=h_w[:, e, :].bitcast(FP8X4), rhs_scale=h_s[:, e, :],
+                    start=e == 0, stop=e == 1,
                 )
             groups = 2 // len(banks)
             for g0, bank in enumerate(banks):
                 res = ring.tile([P, groups, width], F32, name="res", tag="res", bufs=4)
-                nc.scalar.activation(out=res[:], in_=bank[:], func=SIGMOID)
+                nc.scalar.activation(out=res[:].rearrange("p g j -> p (g j)"), in_=bank, func=SIGMOID)
                 queue = nc.scalar if (c, g0) == (LAST, 1) else nc.sync
                 queue.dma_start(out=out_v[:, g0 : g0 + groups, c * CHUNK : c * CHUNK + width], in_=res[:])
 
@@ -292,33 +275,33 @@ def tile_list_ckg_sig_kernel(
         for i in range(2):
             cast(nc.scalar.copy, i, 0, P)
             quantize_weight(i)
-        cast(nc.vector.tensor_copy, 2, 0, VECTOR_CAST)
-        cast(nc.scalar.copy, 2, VECTOR_CAST, P)
+        shared_cast(2)
         quantize_weight(2)
         we_w = [kept([P, R], I32, f"we_w{e}", ("raw1", "grouped1")[e]) for e in range(2)]
         nc.sync.dma_start(out=we_w[0][:], in_=as_words(wer_words))
         nc.sync.dma_start(out=we_w[1][:], in_=as_words(wei_words))
-        cast(nc.vector.tensor_copy, 3, 0, VECTOR_CAST)
-        cast(nc.scalar.copy, 3, VECTOR_CAST, P)
+        shared_cast(3)
         quantize_weight(3)
-        nc.vector.tensor_copy(out=we_dealt_s[:], in_=we_s[:].rearrange("p (m t) -> p t m", t=4))
+        nc.vector.tensor_copy(
+            out=we_dealt_s[:].rearrange("p (t m) -> p t m", t=4), in_=we_s[:].rearrange("p (m t) -> p t m", t=4)
+        )
 
-        arr_bank = turned_relation(0, 0)
-        arr0 = kept([P, R], F32, "arr0", "raw3")
-        nc.scalar.copy(out=arr0[:], in_=arr_bank[:])
-        ari0 = turned_relation(0, 1)
+        arr0 = kept([P, R], F32, "arr0", "raw3")[:]
+        nc.scalar.copy(out=arr0, in_=turned_relation(0, 0, score_bank("arr0")))
+        ari0 = turned_relation(0, 1, relation_bank("ari0", 1, 0))
 
         gather_table_words(0)
         gather_table_words(1)
-        deal_words(0)
-        aer0 = turned_entity(0, 0, kept([P, R], F32, "aer0")[:])
-        deal_words(1)
-        aei0 = turned_entity(0, 1, kept([P, R], F32, "aei0")[:])
+        ae0 = [kept([P, R], F32, f"ae0_{e}") for e in range(2)]
+        for e in range(2):
+            deal_words(e)
+            bank = turned_entity(0, e, entity_bank("ae0_bank"), we_w[e], we_s)
+            nc.scalar.copy(out=ae0[e][:].rearrange("p (t m) -> p t m", t=4), in_=bank.rearrange("p (m t) -> p t m", t=4))
         first = [kept([P, R], F32, f"first{n}") for n in range(4)]
-        nc.gpsimd.tensor_tensor(out=first[0][:], in0=aer0, in1=arr0[:], op=MULT)
-        nc.vector.tensor_tensor(out=first[2][:], in0=aer0, in1=ari0[:], op=MULT)
-        nc.vector.scalar_tensor_tensor(out=first[1][:], in0=aei0, scalar=-1.0, in1=ari0[:], op0=MULT, op1=MULT)
-        nc.gpsimd.tensor_tensor(out=first[3][:], in0=aei0, in1=arr0[:], op=MULT)
+        nc.gpsimd.tensor_tensor(out=first[0][:], in0=ae0[0][:], in1=arr0, op=MULT)
+        times(first[2][:], ae0[0][:], ari0)
+        minus_times(first[1][:], ae0[1][:], ari0)
+        nc.gpsimd.tensor_tensor(out=first[3][:], in0=ae0[1][:], in1=arr0, op=MULT)
         entity(1)
         entity(2)
 
@@ -331,7 +314,7 @@ def tile_list_ckg_sig_kernel(
                 load_scale_rows(n_s[:, e, :], 0, r, scales[0])
 
         first_two = kept([P, 2, 2 * CHUNK, 4], BF16, "first_two")
-        hb = {c: first_two[:, :, c * CHUNK : (c + 1) * CHUNK] for c in range(2)}
+        hb = {c: first_two[:, :, cols(c)] for c in range(2)}
         for c in range(1, LAST):
             with_arr, with_ari = products(c)
             if c > LAG:
@@ -341,21 +324,24 @@ def tile_list_ckg_sig_kernel(
             if c <= 2:
                 add_by_transposes(0, c - 1, first[2 * c - 2], first[2 * c - 1])
             if c + AHEAD == LAST:
-                pair = kept([P, 2, R], F32, "ae_last")
-                aer, aei = [turned_entity(LAST, e, pair[:, e]) for e in range(2)]
+                ae_last = kept([P, 2, R], F32, "ae_last")
+                for e in range(2):
+                    bank = turned_entity(LAST, e, relation_bank("ae_last_bank", e, 1), we_dealt_w[e], we_dealt_s)
+                    nc.scalar.copy(out=ae_last[:, e], in_=bank)
             if c > 1:
                 hb[c] = ring.tile([P, 2, CHUNK, 4], BF16, name="hb", bufs=LAG + 2, align_bytes=64)
             for part in (slice(1, 2), slice(0, 1)) if c == 1 else (slice(0, 2),):
                 nc.gpsimd.tensor_tensor(out=hb[c][:, part], in0=with_arr[:, part], in1=with_ari[:, part], op=ADD)
 
-        arr, ari = [turned_relation(LAST, e) for e in range(2)]
+        aer, aei = ae_last[:, 0], ae_last[:, 1]
+        arr, ari = [turned_relation(LAST, e, relation_bank("ar_last", e, 0)) for e in range(2)]
         with_arr, with_ari = [ring.tile([P, 2, R], F32, name=f"prod{e}") for e in range(2)]
         hb[LAST] = kept([P, 2, CHUNK, 4], BF16, "hb_last")
-        nc.vector.tensor_tensor(out=with_arr[:, 0], in0=aer, in1=arr[:], op=MULT)
-        nc.vector.scalar_tensor_tensor(out=with_ari[:, 0], in0=aei, scalar=-1.0, in1=ari[:], op0=MULT, op1=MULT)
-        nc.vector.tensor_tensor(out=with_arr[:, 1], in0=aei, in1=arr[:], op=MULT)
-        for cols in (slice(0, R // 2), slice(R // 2, R)):
-            nc.vector.tensor_tensor(out=with_ari[:, 1, cols], in0=aer[:, cols], in1=ari[:, cols], op=MULT)
+        times(with_arr[:, 0], aer, arr)
+        minus_times(with_ari[:, 0], aei, ari)
+        times(with_arr[:, 1], aei, arr)
+        for half in (slice(0, R // 2), slice(R // 2, R)):
+            times(with_ari[:, 1, half], aer[:, half], ari[:, half])
         for part in range(2):
             add_by_transposes(LAST, part, with_arr[:, part], with_ari[:, part])
         for c in range(LAST - LAG, CHUNKS):

from contextlib import ExitStack

import concourse.mybir as mybir
from concourse.masks import make_identity

K, L, R, N, T, J = 512, 1024, 512, 256, 2048, 1024
FLOPS = 2 * J * (2 * K * R + 2 * L * R + 2 * R * N)

F32 = mybir.dt.float32
BF16 = mybir.dt.bfloat16
I32 = mybir.dt.int32
U32 = mybir.dt.uint32
U16 = mybir.dt.uint16
U8 = mybir.dt.uint8
FP8X4 = mybir.dt.float8_e4m3fn_x4
FP4X4 = mybir.dt.float4_e2m1fn_x4
MULT = mybir.AluOpType.mult
ADD = mybir.AluOpType.add
SIGMOID = mybir.ActivationFunctionType.Sigmoid

P = 128
QUAD = 32
CHUNK = 128
CHUNKS = J // CHUNK
LAST = CHUNKS - 1
FIRST_GATHER = 2 * CHUNK
AHEAD = 2
LAG = 2
LANDING = 96
ENTITY_ROWS = 8
VECTOR_CAST = {2: 3 * P // 8, 3: 5 * P // 8}


def tile_list_ckg_sig_kernel(
    tc, tab_words, tab_scales, tab2_words, tab2_scales, wer_words, wer_scales, wei_words, wei_scales,
    wrr, wri, nr_words, nr_scales, ni_words, ni_scales, offs, offs2, out,
):
    nc = tc.nc
    with ExitStack() as ctx:
        keep = ctx.enter_context(tc.tile_pool(name="keep", bufs=1))
        ring = ctx.enter_context(tc.tile_pool(name="ring", bufs=3))
        psum = ctx.enter_context(tc.psum_pool(name="psum", bufs=1))

        def kept(shape, dtype, name, tag=None):
            return keep.tile(shape, dtype, name=name, tag=tag or name, align_bytes=64)

        def entity_bank(name):
            return psum.tile([P, R], F32, name=name, tag="entity_bank", bufs=3)

        def relation_bank(name, e, turn):
            return psum.tile([P, R], F32, name=name, tag=f"relation_bank{e}_{turn}")

        def score_bank(name):
            return psum.tile([P, R], F32, name=name, tag="score_bank")

        def cols(c):
            return slice(c * CHUNK, (c + 1) * CHUNK)

        def by_entry(ap):
            return ap.rearrange("p (t j) -> p j t", t=4)

        list1 = keep.tile([P, J // 16], U16, name="list1")
        list2 = keep.tile([P, J // 16], U16, name="list2")
        tab_w = kept([P, T], U32, "tab_w")
        tab_s = kept([P, T], U8, "tab_s")
        tab2_w = kept([P, T], U32, "tab2_w")
        tab2_s = kept([P, T], U8, "tab2_s")
        we_s = kept([P, R], U8, "we_s")
        raw = [kept([P, 4, R], F32, f"raw{i}") for i in range(4)]
        v2_s = [kept([P, J], U8, f"v2_s{a}") for a in range(2)]
        ident = kept([P, P], F32, "ident")

        nc.gpsimd.memset(tab2_s[0:LANDING].bitcast(I32), 0)
        nc.gpsimd.memset(we_s[:].bitcast(I32), 0)
        warm = kept([P, 2], F32, "warm")
        nc.gpsimd.memset(warm[:, 0:1], 0.0)
        nc.scalar.activation(out=warm[:, 1:2], in_=warm[:, 0:1], func=SIGMOID)
        nc.vector.memset(tab_s[:].bitcast(I32), 0)
        for a in range(2):
            nc.vector.memset(v2_s[a][:].bitcast(I32), 0)

        def as_words(words):
            return words[0].rearrange("p c i -> p (c i)").bitcast(I32)

        def load_float_pass(i):
            rows = (wrr, wri)[i // 2][512 * (i % 2) : 512 * (i % 2 + 1), :]
            nc.sync.dma_start(out=raw[i][:], in_=rows.rearrange("(p j) c -> p j c", j=4))

        def load_scale_rows(dst, first, r, rows):
            nc.sync.dma_start(out=dst[first + r : P : QUAD].bitcast(I32), in_=rows[r:16:4].bitcast(I32))

        picked2 = kept([P, J], U8, "picked2")

        def move_scale_rows(a):
            for r in range(4):
                first = LANDING + 16 * a + r
                nc.sync.dma_start(
                    out=v2_s[a][r:P:QUAD].bitcast(I32), in_=picked2[first : first + 13 : 4].bitcast(I32)
                )

        nc.sync.dma_start(list2[:], offs2)
        nc.sync.dma_start(
            out=tab2_s[LANDING:P].bitcast(I32), in_=tab2_scales.rearrange("a q t -> (a q) t").bitcast(I32)
        )
        nc.sync.dma_start(out=tab2_w[:].bitcast(I32), in_=as_words(tab2_words))
        load_float_pass(0)
        nc.sync.dma_start(list1[:], offs)
        for r in range(4):
            load_scale_rows(tab_s, ENTITY_ROWS, r, tab_scales[0])
        load_float_pass(1)
        nc.vector.tensor_copy(picked2[:], tab2_s[:].indirect(list2[:]))
        for a in range(2):
            move_scale_rows(a)
            for r in (2 * a, 2 * a + 1):
                load_scale_rows(we_s, 0, r, wer_scales[0])
            load_float_pass(2 + a)
        for r in range(4):
            load_scale_rows(we_s, ENTITY_ROWS, r, wei_scales[0])
        nc.sync.dma_start(out=tab_w[:].bitcast(I32), in_=as_words(tab_words))
        make_identity(nc, ident[:])

        v_s = kept([P, J], U8, "v_s")
        v_w = {}
        v2_both = kept([P, J], U32, "v2_both")
        v2_w = kept([P, 2, J], U16, "v2_w")
        we_dealt_w = [kept([P, R], U32, f"we_dealt_w{e}") for e in range(2)]
        we_dealt_s = kept([P, R], U8, "we_dealt_s")
        grouped = [kept([P, 4, P, 4], BF16, f"grouped{i}") for i in range(4)]
        wr_w = {}
        wr_s = [kept([P, R], U8, f"wr_s{i}") for i in range(4)]

        def cast(copy, i, m0, m1):
            copy(
                out=grouped[i][:, :, m0:m1, :].rearrange("p t m j -> p m j t"),
                in_=raw[i][:].rearrange("p j (m t) -> p m j t", t=4)[:, m0:m1, :, :],
            )

        def shared_cast(i):
            cast(nc.vector.tensor_copy, i, 0, VECTOR_CAST[i])
            cast(nc.scalar.copy, i, VECTOR_CAST[i], P)

        def quantize_weight(i):
            wr_w[i] = kept([P, R], U32, f"wr_w{i}", "tab_s" if i == 0 else None)
            nc.vector.quantize_mx(
                out=wr_w[i][:].bitcast(FP8X4), scales=wr_s[i][:], in_=grouped[i][:].rearrange("p t m j -> p (t m j)")
            )

        def deal_words(e):
            nc.scalar.copy(
                out=we_dealt_w[e][:].rearrange("p (t g i) -> p g t i", t=4, i=4),
                in_=we_w[e][:].bitcast(U32).rearrange("p (g i t) -> p g t i", i=4, t=4),
            )

        def gather_table_words(piece):
            j0, j1 = ((0, FIRST_GATHER), (FIRST_GATHER, J))[piece]
            v_w[piece] = kept([P, j1 - j0], U32, f"v_w{piece}")
            nc.vector.tensor_copy(v_w[piece][:], tab_w[:].indirect(list1[:, j0 // 16 : j1 // 16]))

        def entity_columns(c):
            piece, j0 = (0, c * CHUNK) if c * CHUNK < FIRST_GATHER else (1, c * CHUNK - FIRST_GATHER)
            return v_w[piece][:, j0 : j0 + CHUNK].bitcast(FP8X4), v_s[ENTITY_ROWS:, cols(c)]

        ae = {}

        def entity(c):
            words, scales = entity_columns(c)
            pair = ring.tile([P, 2, CHUNK, 4], F32, name="ae", bufs=AHEAD)
            ae[c] = [pair[:, 0], pair[:, 1], pair[:]]
            for e in range(2):
                bank = entity_bank("ae_bank")
                for t in range(4):
                    nc.tensor.matmul_mx(
                        out=bank[:, cols(t)], lhsT=we_dealt_w[e][:, cols(t)].bitcast(FP8X4),
                        lhsT_scale=we_dealt_s[ENTITY_ROWS * e :, cols(t)], rhs=words, rhs_scale=scales,
                        start=True, stop=True,
                    )
                nc.scalar.copy(out=ae[c][e], in_=by_entry(bank[:]))

        def relation(c, e):
            bank = relation_bank("ar_bank", e, c % 2)
            for a in range(2):
                for t in range(4):
                    nc.tensor.matmul_mx(
                        out=bank[:, cols(t)], lhsT=wr_w[2 * e + a][:, cols(t)].bitcast(FP8X4),
                        lhsT_scale=wr_s[2 * e + a][:, cols(t)], rhs=v2_w[:, a, cols(c)].bitcast(FP4X4),
                        rhs_scale=v2_s[a][:, cols(c)], start=(a, t) == (0, 0), stop=(a, t) == (1, 3),
                    )
            return by_entry(bank[:])

        def times(out, first, second):
            nc.vector.tensor_tensor(out=out, in0=first, in1=second, op=MULT)

        def minus_times(out, first, second):
            nc.vector.scalar_tensor_tensor(out=out, in0=first, scalar=-1.0, in1=second, op0=MULT, op1=MULT)

        def products(c):
            aer, aei, pair = ae[c]
            arr, ari = [relation(c, e) for e in range(2)]
            with_arr, with_ari = [ring.tile([P, 2, CHUNK, 4], F32, name=f"prod{e}") for e in range(2)]
            if c == 1:
                times(with_arr[:, 0], aer, arr)
                times(with_ari[:, 1], aer, ari)
                times(with_arr[:, 1], aei, arr)
            else:
                times(with_arr[:], pair, arr.unsqueeze(1).to_broadcast([P, 2, CHUNK, 4]))
                times(with_ari[:, 1], aer, ari)
            minus_times(with_ari[:, 0], aei, ari)
            return with_arr, with_ari

        def turned_relation(c, e, bank):
            for a in range(2):
                nc.tensor.matmul_mx(
                    out=bank[:], lhsT=v2_w[:, a, cols(c)].bitcast(FP4X4), lhsT_scale=v2_s[a][:, cols(c)],
                    rhs=wr_w[2 * e + a][:].bitcast(FP8X4), rhs_scale=wr_s[2 * e + a][:], start=a == 0, stop=a == 1,
                )
            return bank[:]

        def turned_entity(c, e, bank, weight_words, weight_scales):
            words, scales = entity_columns(c)
            nc.tensor.matmul_mx(
                out=bank[:], lhsT=words, lhsT_scale=scales, rhs=weight_words[:].bitcast(FP8X4),
                rhs_scale=weight_scales[ENTITY_ROWS * e :], start=True, stop=True,
            )
            return bank[:]

        def add_by_transposes(c, part, first, second):
            bank = entity_bank("sum_bank")
            for n, prod in enumerate((first, second)):
                for t in range(4):
                    nc.tensor.matmul(
                        out=bank[:, cols(t)], lhsT=prod[:, cols(t)], rhs=ident[:],
                        is_transpose=True, start=(n, t) == (0, 0), stop=(n, t) == (1, 3),
                    )
            nc.scalar.copy(out=hb[c][:, part], in_=by_entry(bank[:]))

        out_v = out.rearrange("(g p) j -> p g j", p=P)

        def score(c):
            width = 2 * CHUNK if c == 0 else CHUNK
            rounded = first_two if c == 0 else hb[c]
            h_w = ring.tile([P, 2, width], U32, name="h_w", align_bytes=64)
            h_s = ring.tile([P, 2, width], U8, name="h_s", align_bytes=64)
            for part in (slice(0, 1), slice(1, 2)) if c == LAST else (slice(0, 2),):
                nc.vector.quantize_mx(
                    out=h_w[:, part].rearrange("p e j -> p (e j)").bitcast(FP8X4),
                    scales=h_s[:, part].rearrange("p e j -> p (e j)"),
                    in_=rounded[:, part].rearrange("p e j t -> p (e j t)"),
                )
            if c == LAST:
                banks = [relation_bank("y_last", 0, g)[:, 0:width] for g in range(2)]
                sums = banks
                order = [(g, e) for e in range(2) for g in range(2)]
            else:
                bank = relation_bank("y_bank", 1, 1) if c == LAST - 1 else score_bank("y_bank")
                banks = [bank[:, 0 : 2 * width]]
                sums = [bank[:, g * width : (g + 1) * width] for g in range(2)]
                order = [(g, e) for g in range(2) for e in range(2)]
            for g, e in order:
                nc.tensor.matmul_mx(
                    out=sums[g], lhsT=n_w[:, e, 2 * P * g : 2 * P * (g + 1)].bitcast(FP4X4),
                    lhsT_scale=n_s[:, e, cols(g)], rhs=h_w[:, e, :].bitcast(FP8X4), rhs_scale=h_s[:, e, :],
                    start=e == 0, stop=e == 1,
                )
            groups = 2 // len(banks)
            for g0, bank in enumerate(banks):
                res = ring.tile([P, groups, width], F32, name="res", tag="res", bufs=4)
                nc.scalar.activation(out=res[:].rearrange("p g j -> p (g j)"), in_=bank, func=SIGMOID)
                queue = nc.scalar if (c, g0) == (LAST, 1) else nc.sync
                queue.dma_start(out=out_v[:, g0 : g0 + groups, c * CHUNK : c * CHUNK + width], in_=res[:])

        nc.vector.tensor_copy(v2_both[:], tab2_w[:].indirect(list2[:]))
        nc.vector.tensor_copy(v_s[:], tab_s[:].indirect(list1[:]))
        nc.vector.tensor_copy(out=v2_w[:], in_=v2_both[:].bitcast(U16).rearrange("p (j d) -> p d j", d=2))

        for i in range(2):
            cast(nc.scalar.copy, i, 0, P)
            quantize_weight(i)
        shared_cast(2)
        quantize_weight(2)
        we_w = [kept([P, R], I32, f"we_w{e}", ("raw1", "grouped1")[e]) for e in range(2)]
        nc.sync.dma_start(out=we_w[0][:], in_=as_words(wer_words))
        nc.sync.dma_start(out=we_w[1][:], in_=as_words(wei_words))
        shared_cast(3)
        quantize_weight(3)
        nc.vector.tensor_copy(
            out=we_dealt_s[:].rearrange("p (t m) -> p t m", t=4), in_=we_s[:].rearrange("p (m t) -> p t m", t=4)
        )

        arr0 = kept([P, R], F32, "arr0", "raw3")[:]
        nc.scalar.copy(out=arr0, in_=turned_relation(0, 0, score_bank("arr0")))
        ari0 = turned_relation(0, 1, relation_bank("ari0", 1, 0))

        gather_table_words(0)
        gather_table_words(1)
        ae0 = [kept([P, R], F32, f"ae0_{e}") for e in range(2)]
        for e in range(2):
            deal_words(e)
            bank = turned_entity(0, e, entity_bank("ae0_bank"), we_w[e], we_s)
            nc.scalar.copy(out=ae0[e][:].rearrange("p (t m) -> p t m", t=4), in_=bank.rearrange("p (m t) -> p t m", t=4))
        first = [kept([P, R], F32, f"first{n}") for n in range(4)]
        nc.gpsimd.tensor_tensor(out=first[0][:], in0=ae0[0][:], in1=arr0, op=MULT)
        times(first[2][:], ae0[0][:], ari0)
        minus_times(first[1][:], ae0[1][:], ari0)
        nc.gpsimd.tensor_tensor(out=first[3][:], in0=ae0[1][:], in1=arr0, op=MULT)
        entity(1)
        entity(2)

        n_w = kept([P, 2, 2 * N], U8, "n_w", "grouped3")
        n_s = kept([P, 2, N], U8, "n_s", "raw1")
        nc.gpsimd.memset(n_s[:].rearrange("p e n -> p (e n)").bitcast(I32), 0)
        for e, (words, scales) in enumerate(((nr_words, nr_scales), (ni_words, ni_scales))):
            nc.sync.dma_start(out=n_w[:, e, :].bitcast(I32), in_=words[0].bitcast(I32))
            for r in range(4):
                load_scale_rows(n_s[:, e, :], 0, r, scales[0])

        first_two = kept([P, 2, 2 * CHUNK, 4], BF16, "first_two")
        hb = {c: first_two[:, :, cols(c)] for c in range(2)}
        for c in range(1, LAST):
            with_arr, with_ari = products(c)
            if c > LAG:
                score(0 if c == LAG + 1 else c - LAG)
            if c + AHEAD < LAST:
                entity(c + AHEAD)
            if c <= 2:
                add_by_transposes(0, c - 1, first[2 * c - 2], first[2 * c - 1])
            if c + AHEAD == LAST:
                ae_last = kept([P, 2, R], F32, "ae_last")
                for e in range(2):
                    bank = turned_entity(LAST, e, relation_bank("ae_last_bank", e, 1), we_dealt_w[e], we_dealt_s)
                    nc.scalar.copy(out=ae_last[:, e], in_=bank)
            if c > 1:
                hb[c] = ring.tile([P, 2, CHUNK, 4], BF16, name="hb", bufs=LAG + 2, align_bytes=64)
            for part in (slice(1, 2), slice(0, 1)) if c == 1 else (slice(0, 2),):
                nc.gpsimd.tensor_tensor(out=hb[c][:, part], in0=with_arr[:, part], in1=with_ari[:, part], op=ADD)

        aer, aei = ae_last[:, 0], ae_last[:, 1]
        arr, ari = [turned_relation(LAST, e, relation_bank("ar_last", e, 0)) for e in range(2)]
        with_arr, with_ari = [ring.tile([P, 2, R], F32, name=f"prod{e}") for e in range(2)]
        hb[LAST] = kept([P, 2, CHUNK, 4], BF16, "hb_last")
        times(with_arr[:, 0], aer, arr)
        minus_times(with_ari[:, 0], aei, ari)
        times(with_arr[:, 1], aei, arr)
        for half in (slice(0, R // 2), slice(R // 2, R)):
            times(with_ari[:, 1, half], aer[:, half], ari[:, half])
        for part in range(2):
            add_by_transposes(LAST, part, with_arr[:, part], with_ari[:, part])
        for c in range(LAST - LAG, CHUNKS):
            score(c)
